import numpy as np
import ml_dtypes


def mxq(x, axis, fmt="e4m3"):
    dtype, down = {"e4m3": (ml_dtypes.float8_e4m3fn, 7), "e5m2": (ml_dtypes.float8_e5m2, 14)}[fmt]
    v = np.moveaxis(np.asarray(x, np.float32).astype(ml_dtypes.bfloat16).astype(np.float64), axis, -1)
    blocks = v.reshape(v.shape[:-1] + (-1, 32))
    amax = np.abs(blocks).max(-1, keepdims=True)
    byte = np.maximum(np.where(amax > 0, np.frexp(amax)[1] - 1 + 127, 0) - down, 1)
    scale = np.exp2(byte - 127.0)
    codes = (blocks / scale).astype(np.float32).astype(dtype).astype(np.float64)
    return np.moveaxis((codes * scale).reshape(v.shape), -1, axis)


WIDE = False


def mx_kscale(k):
    if not WIDE:
        return np.ones(k)
    levels = np.array([10, -10, 5, -5, 0])
    if k % 512:
        return np.exp2(np.random.permutation(np.resize(levels, k // 32))).repeat(32)
    a = np.empty((k // 512, 16))
    for p in range(k // 512):
        a[p, :8] = np.random.permutation(np.resize(levels, 8))
        for g in range(8):
            far = levels[np.abs(levels - a[p, g]) >= 10]
            a[p, g + 8] = far[np.random.randint(len(far))]
    return np.exp2(a.ravel()).repeat(32)


def f64(x):
    return np.asarray(x).astype(np.float64)


def striped(idx):
    return np.tile(idx.reshape(-1, 16).T, (8, 1)).astype(np.uint16)


def unstriped(offs):
    return offs[:16].T.reshape(-1).astype(np.int64)


def striped8(idx):
    return np.concatenate([x.reshape(-1, 16).T for x in idx]).astype(np.uint16)


def runs(offs, k):
    lists = np.stack([offs[16 * r : 16 * r + 16].T.reshape(-1) for r in range(8)]).astype(np.int64)
    return lists[np.arange(k) % 512 // 64]


def pack_weight(w):
    k, n = w.shape
    w = f64(np.asarray(w, np.float32).astype(ml_dtypes.bfloat16)).reshape(k // 32, 32, n)
    amax = np.abs(w).max(1)
    byte = np.clip(np.where(amax > 0, np.frexp(amax)[1] - 1 + 127 - 7, 1), 1, 254)
    scaled = (w * np.exp2(127.0 - byte)[:, None, :]).reshape(k, n).astype(np.float32)
    words = np.ascontiguousarray(scaled.reshape(k // 512, 128, 4, n).transpose(0, 1, 3, 2)).astype(ml_dtypes.float8_e4m3fn).view(np.uint8)
    return words, np.ascontiguousarray(byte.astype(np.uint8).reshape(k // 512, 16, n))


def unpack_weight(words, scales):
    g, p, n, _ = words.shape
    vals = np.ascontiguousarray(words).view(ml_dtypes.float8_e4m3fn).astype(np.float64) * np.repeat(np.exp2(scales.astype(np.float64) - 127.0), 8, axis=1)[..., None]
    return vals.transpose(0, 1, 3, 2).reshape(g * 512, n)


def sigmoid(v):
    return 1.0 / (1.0 + np.exp(-np.maximum(v, -700.0)))


K, T, S, V, H = 512, 2048, 512, 512, 512


def setup_inputs():
    n = np.random.standard_normal
    s = mx_kscale(K)[:, None]
    u = mx_kscale(S)
    packed_xT = pack_weight(n((K, T)) * s)
    return {
        "x_words": packed_xT[0],
        "x_scales": packed_xT[1],
        "w1": (n((K, H)) / np.sqrt(K) / s).astype(np.float32),
        "w2": (n((K, H)) / np.sqrt(K) / s).astype(np.float32),
        "w3": (n((K, H)) / np.sqrt(K) / s).astype(np.float32),
        "ga": (np.random.uniform(0.5, 1.5, (H, 1)) * u[:, None]).astype(np.float32),
        "gb": (np.random.uniform(0.5, 1.5, (H, 1)) / u[:, None]).astype(np.float32),
        "offs": striped(np.random.permutation(T)[:S]),
        "two": striped(np.random.permutation(T)[:S]),
        "n1": striped8(np.stack([np.random.permutation(S) for _ in range(8)])),
        "n2": striped8(np.stack([np.random.permutation(S) for _ in range(8)])),
        "three": striped(np.random.permutation(T)[:V]),
        "n3": striped8(np.stack([np.random.permutation(V) for _ in range(8)])),
        "n4": striped8(np.stack([np.random.permutation(V) for _ in range(8)])),
        "n5": striped8(np.stack([np.random.permutation(V) for _ in range(8)])),
        "n6": striped8(np.stack([np.random.permutation(V) for _ in range(8)])),
        "n7": striped8(np.stack([np.random.permutation(V) for _ in range(8)])),
    }


def reference(x_words, x_scales, w1, w2, w3, ga, gb, offs, two, n1, n2, three, n3, n4, n5, n6, n7):
    xq = unpack_weight(x_words, x_scales)[:, unstriped(offs)]
    y = mxq(f64(w1), 0, "e4m3").T @ xq
    x_two = unpack_weight(x_words, x_scales)[:, unstriped(two)]
    d = mxq(f64(w2), 0, "e4m3").T @ x_two
    z = f64(ga) * ((y + y[np.arange(H)[:, None], runs(n1, H)]) * (sigmoid(d + d[np.arange(H)[:, None], runs(n2, H)])))
    x_three = unpack_weight(x_words, x_scales)[:, unstriped(three)]
    b = mxq(f64(w3), 0, "e4m3").T @ x_three
    sm = np.maximum(b, b[np.arange(H)[:, None], runs(n4, H)])
    ds = np.zeros((H, V))
    ds[np.arange(H)[:, None], runs(n3, H)] = sm
    z2 = f64(gb) * (ds * sigmoid(b))
    s = 0.0625 * ((mxq(z, 0, "e4m3").T @ mxq(z2, 0, "e4m3")))
    return (s[np.arange(S)[:, None], runs(n5, S)]) * sigmoid(s) + (s[np.arange(S)[:, None], runs(n6, S)]) * (sigmoid(s[np.arange(S)[:, None], runs(n7, S)]))

@@ -1,0 +1,252 @@
+from contextlib import ExitStack
+
+import concourse.mybir as mybir
+from concourse.masks import make_identity
+
+F32 = mybir.dt.float32
+BF16 = mybir.dt.bfloat16
+I32 = mybir.dt.int32
+U32 = mybir.dt.uint32
+U16 = mybir.dt.uint16
+U8 = mybir.dt.uint8
+FP8X4 = mybir.dt.float8_e4m3fn_x4
+ACT = mybir.ActivationFunctionType
+ALU = mybir.AluOpType
+
+P = 128
+PACK = 4
+T = 2048
+W = 512
+HALF = W // 2
+LIST_COLS = W // 16
+
+FLOPS = 4 * 2 * 512 * 512 * 512
+
+
+def tile_picked_twktriebsendgwsum_none_p_kernel(
+    tc, x_words, x_scales, w1, w2, w3, ga, gb, offs, two, n1, n2, three, n3, n4, n5, n6, n7, out
+):
+    nc = tc.nc
+    with ExitStack() as ctx:
+        lists = ctx.enter_context(tc.tile_pool(name="lists", bufs=1))
+        keep = ctx.enter_context(tc.tile_pool(name="keep", bufs=1))
+        psum = ctx.enter_context(tc.psum_pool(name="psum", bufs=1))
+
+        def bank(i):
+            return psum.tile([P, W], F32, name="bank%d" % i, tag="bank%d" % i)
+
+        def load_list(src, name):
+            tile = lists.tile([P, LIST_COLS], U16, name=name)
+            nc.sync.dma_start(tile[:], src)
+            return tile
+
+        def load_weight(src, name):
+            raw = keep.tile([P, PACK, W], F32, name=name)
+            nc.sync.dma_start(raw[:], src.rearrange("(p j) c -> p j c", j=PACK))
+            return raw
+
+        def halves(offsets):
+            return [
+                (slice(h * HALF, (h + 1) * HALF), offsets[:, h * LIST_COLS // 2 : (h + 1) * LIST_COLS // 2])
+                for h in range(2)
+            ]
+
+        table_scales = keep.tile([P, T], U8, name="table_scales", align_bytes=64)
+        nc.gpsimd.memset(table_scales[:].bitcast(I32), 0)
+        three_t = load_list(three, "three_t")
+        for q in range(4):
+            nc.scalar.dma_start(
+                table_scales[32 * q : 32 * q + 4, :].bitcast(I32), x_scales[0, 4 * q : 4 * q + 4, :].bitcast(I32)
+            )
+        table_words = keep.tile([P, T], U32, name="table_words", align_bytes=64)
+        nc.sync.dma_start(table_words[:].bitcast(I32), x_words[0].rearrange("p n t -> p (n t)").bitcast(I32))
+        two_t = load_list(two, "two_t")
+        offs_t = load_list(offs, "offs_t")
+        w3_raw = load_weight(w3, "w3_raw")
+        n4_t = load_list(n4, "n4_t")
+        n3_t = load_list(n3, "n3_t")
+        w2_raw = load_weight(w2, "w2_raw")
+        n2_t = load_list(n2, "n2_t")
+        w1_raw = load_weight(w1, "w1_raw")
+        n1_t = load_list(n1, "n1_t")
+        ga_t = keep.tile([P, PACK], F32, name="ga_t")
+        nc.sync.dma_start(ga_t[:], ga.rearrange("(p t) o -> p (t o)", t=PACK))
+        gb_t = keep.tile([P, PACK], F32, name="gb_t")
+        nc.sync.dma_start(gb_t[:], gb.rearrange("(p t) o -> p (t o)", t=PACK))
+        n5_t = load_list(n5, "n5_t")
+        n6_t = load_list(n6, "n6_t")
+        n7_t = load_list(n7, "n7_t")
+
+        ident = keep.tile([P, P], F32, name="ident")
+        make_identity(nc, ident[:])
+        warm = keep.tile([P, 1], F32, name="warm")
+        nc.scalar.activation(warm[:], ident[:, 0:1], ACT.Sigmoid)
+
+        def pick_scales(offsets, name):
+            picked = keep.tile([P, W], U8, name=name, align_bytes=64)
+            nc.vector.tensor_copy(picked[:], table_scales[:].indirect(offsets[:]))
+            return picked
+
+        def pick_words(offsets, name):
+            picked = keep.tile([P, W], U32, name=name, align_bytes=64)
+            nc.vector.tensor_copy(picked[:], table_words[:].indirect(offsets[:]))
+            return picked
+
+        def quantize(grouped, name):
+            codes = keep.tile([P, W], U32, name=name + "_codes", align_bytes=64)
+            scales = keep.tile([P, W], U8, name=name + "_scales", align_bytes=64)
+            nc.vector.quantize_mx(out=codes[:].bitcast(FP8X4), scales=scales[:], in_=grouped[:])
+            return codes, scales
+
+        def group_weight(raw, name):
+            grouped = keep.tile([P, PACK * W], BF16, name=name + "_grouped", align_bytes=64)
+            nc.scalar.copy(
+                grouped[:].rearrange("p (t m j) -> p m j t", t=PACK, j=PACK),
+                raw[:].rearrange("p j (m t) -> p m j t", t=PACK),
+            )
+            return grouped
+
+        def product(acc, stationary, t, moving):
+            cols = slice(t * P, (t + 1) * P)
+            nc.tensor.matmul_mx(
+                out=acc[:],
+                lhsT=stationary[0][:, cols].bitcast(FP8X4),
+                lhsT_scale=stationary[1][:, cols],
+                rhs=moving[0][:].bitcast(FP8X4),
+                rhs_scale=moving[1][:],
+                start=True,
+                stop=True,
+            )
+
+        xs3 = pick_scales(three_t, "xs3")
+        xs2 = pick_scales(two_t, "xs2")
+        xs1 = pick_scales(offs_t, "xs1")
+        xw3 = pick_words(three_t, "xw3")
+        w3_q = quantize(group_weight(w3_raw, "w3"), "w3")
+        xw2 = pick_words(two_t, "xw2")
+        xw1 = pick_words(offs_t, "xw1")
+
+        b_win, b_plain, b_sig, b_rise = [], [], [], []
+        for t in range(PACK):
+            acc = bank(t)
+            product(acc, w3_q, t, (xw3, xs3))
+            win = keep.tile([P, W], F32, name="b_win%d" % t)
+            nc.scalar.copy(win[:], acc[:])
+            plain = keep.tile([P, W], F32, name="b_plain%d" % t)
+            nc.scalar.copy(plain[:], acc[:])
+            sig = keep.tile([P, W], F32, name="b_sig%d" % t)
+            nc.scalar.activation(sig[:], acc[:], ACT.Sigmoid)
+            diff = keep.tile([P, W], F32, name="b_diff%d" % t)
+            for cols, entries in halves(n4_t):
+                nc.vector.tensor_tensor(diff[:, cols], win[:].indirect(entries), plain[:, cols], ALU.subtract)
+            rise = keep.tile([P, W], F32, name="b_rise%d" % t)
+            nc.scalar.activation(rise[:], diff[:], ACT.Relu)
+            b_plain.append(plain)
+            b_sig.append(sig)
+            b_rise.append(rise)
+
+        w2_q = quantize(group_weight(w2_raw, "w2"), "w2")
+        d_win = []
+        for t in range(PACK):
+            acc = bank(4 + t)
+            product(acc, w2_q, t, (xw2, xs2))
+            win = keep.tile([P, W], F32, name="d_win%d" % t)
+            nc.scalar.copy(win[:], acc[:])
+            d_win.append(win)
+        w1_q = quantize(group_weight(w1_raw, "w1"), "w1")
+        y_win = []
+        for t in range(PACK):
+            acc = bank(t)
+            product(acc, w1_q, t, (xw1, xs1))
+            win = keep.tile([P, W], F32, name="y_win%d" % t)
+            nc.scalar.activation(win[:], acc[:], ACT.Copy, scale=ga_t[:, t : t + 1])
+            y_win.append(win)
+
+        def gather_and_turn(win, offsets, t, banks, name):
+            fetched = keep.tile([P, W], F32, name=name)
+            for cols, entries in halves(offsets):
+                nc.vector.tensor_copy(fetched[:, cols], win[:].indirect(entries))
+            for jb in range(PACK):
+                cols = slice(jb * P, (jb + 1) * P)
+                dst = banks[jb][:, t * P : (t + 1) * P]
+                nc.tensor.matmul(dst, win[:, cols], ident[:], start=True, stop=False, is_transpose=True)
+                nc.tensor.matmul(dst, fetched[:, cols], ident[:], start=False, stop=True, is_transpose=True)
+
+        z2_planes = keep.tile([P, PACK, W], BF16, name="z2_planes")
+        d_banks = [bank(4 + jb) for jb in range(PACK)]
+        y_banks = [bank(jb) for jb in range(PACK)]
+        sent = []
+        for t in range(PACK):
+            ds = keep.tile([P, 2 * W], F32, name="ds%d" % t)
+            nc.vector.tensor_tensor(ds[:].indirect(n3_t[:]), b_rise[t][:], b_plain[t][:], ALU.add)
+            sent.append(ds)
+            gather_and_turn(d_win[t], n2_t, t, d_banks, "d_fetched%d" % t)
+            nc.vector.scalar_tensor_tensor(
+                z2_planes[:, t, :], ds[:, 0:W], gb_t[:, t : t + 1], b_sig[t][:], ALU.mult, ALU.mult
+            )
+        z2_grouped = keep.tile([P, PACK * W], BF16, name="z2_grouped", align_bytes=64)
+        nc.scalar.copy(
+            z2_grouped[:].rearrange("p (c i t) -> p c t i", i=4, t=PACK),
+            z2_planes[:].rearrange("p t (c i) -> p c t i", i=4),
+        )
+        gates = []
+        for jb in range(PACK):
+            gate = keep.tile([P, W], F32, name="gate%d" % jb)
+            nc.scalar.activation(
+                gate[:].rearrange("j (u p e) -> j u p e", u=2, e=2),
+                d_banks[jb][:].rearrange("j (u e p) -> j u p e", u=2, e=2),
+                ACT.Sigmoid,
+            )
+            gates.append(gate)
+        for t in range(PACK):
+            gather_and_turn(y_win[t], n1_t, t, y_banks, "y_fetched%d" % t)
+        z2_q = quantize(z2_grouped, "z2")
+
+        z_grouped = keep.tile([P, PACK * W], BF16, name="z_grouped", align_bytes=64)
+        z_words = z_grouped[:].bitcast(F32).rearrange("p (t m u) -> p t m u", t=PACK, u=2)
+        for jb in range(PACK):
+            z_turned = keep.tile([P, W], BF16, name="z_turned%d" % jb)
+            nc.vector.tensor_tensor(
+                z_turned[:].rearrange("j (u p e) -> j u p e", u=2, e=2),
+                y_banks[jb][:].rearrange("j (u e p) -> j u p e", u=2, e=2),
+                gates[jb][:].rearrange("j (u p e) -> j u p e", u=2, e=2),
+                ALU.mult,
+            )
+            back = bank(4 + jb)
+            pairs = z_turned[:].bitcast(F32)
+            for u in range(2):
+                nc.tensor.transpose(back[:, u * P : (u + 1) * P], pairs[:, u * P : (u + 1) * P], ident[:])
+            nc.scalar.copy(
+                z_words[:, :, 32 * jb : 32 * (jb + 1), :],
+                back[:, 0 : 2 * P].rearrange("p (u m t) -> p t m u", u=2, t=PACK),
+            )
+
+        z_codes = keep.tile([P, W], U32, name="z_codes", align_bytes=64)
+        z_scales = keep.tile([P, W], U8, name="z_scales", align_bytes=64)
+        out_rows = out.rearrange("(p t) v -> p t v", t=PACK)
+        for t in range(PACK):
+            cols = slice(t * P, (t + 1) * P)
+            nc.vector.quantize_mx(
+                out=z_codes[:, cols].bitcast(FP8X4),
+                scales=z_scales[:, cols],
+                in_=z_grouped[:, t * W : (t + 1) * W],
+            )
+        for t in range(PACK):
+            acc = bank(t)
+            product(acc, (z_codes, z_scales), t, z2_q)
+            s_win = keep.tile([P, W], F32, name="s_win%d" % t)
+            nc.scalar.activation(s_win[:], acc[:], ACT.Copy, scale=0.0625)
+            s_sig = keep.tile([P, W], F32, name="s_sig%d" % t)
+            nc.scalar.activation(s_sig[:], acc[:], ACT.Sigmoid, scale=0.0625)
+            s_sig7 = keep.tile([P, W], F32, name="s_sig7_%d" % t)
+            for cols, entries in halves(n7_t):
+                nc.scalar.activation(s_sig7[:, cols], s_win[:].indirect(entries), ACT.Sigmoid)
+            first = keep.tile([P, W], F32, name="first%d" % t)
+            for cols, entries in halves(n5_t):
+                nc.vector.tensor_tensor(first[:, cols], s_win[:].indirect(entries), s_sig[:, cols], ALU.mult)
+            second = keep.tile([P, W], F32, name="second%d" % t)
+            for cols, entries in halves(n6_t):
+                nc.vector.tensor_tensor(second[:, cols], s_win[:].indirect(entries), s_sig7[:, cols], ALU.mult)
+            total = keep.tile([P, W], F32, name="total%d" % t)
+            nc.vector.tensor_tensor(total[:], first[:], second[:], ALU.add)
+            nc.sync.dma_start(out_rows[:, t, :], total[:])

@@ -17,7 +17,6 @@ P = 128
 PACK = 4
 T = 2048
 W = 512
-HALF = W // 2
 LIST_COLS = W // 16
 
 FLOPS = 4 * 2 * 512 * 512 * 512
@@ -40,34 +39,32 @@ def tile_picked_twktriebsendgwsum_none_p_kernel(
             nc.sync.dma_start(tile[:], src)
             return tile
 
-        def load_weight(src, name):
-            raw = keep.tile([P, PACK, W], F32, name=name)
-            nc.sync.dma_start(raw[:], src.rearrange("(p j) c -> p j c", j=PACK))
-            return raw
-
-        def halves(offsets):
-            return [
-                (slice(h * HALF, (h + 1) * HALF), offsets[:, h * LIST_COLS // 2 : (h + 1) * LIST_COLS // 2])
-                for h in range(2)
-            ]
+        def load_weight(src, name, pieces):
+            width = W // pieces
+            parts = []
+            for h in range(pieces):
+                raw = keep.tile([P, PACK, width], F32, name="%s%d" % (name, h))
+                nc.sync.dma_start(raw[:], src.rearrange("(p j) c -> p j c", j=PACK)[:, :, h * width : (h + 1) * width])
+                parts.append(raw)
+            return parts
 
         table_scales = keep.tile([P, T], U8, name="table_scales", align_bytes=64)
         nc.gpsimd.memset(table_scales[:].bitcast(I32), 0)
         three_t = load_list(three, "three_t")
+        two_t = load_list(two, "two_t")
+        offs_t = load_list(offs, "offs_t")
         for q in range(4):
-            nc.scalar.dma_start(
+            nc.sync.dma_start(
                 table_scales[32 * q : 32 * q + 4, :].bitcast(I32), x_scales[0, 4 * q : 4 * q + 4, :].bitcast(I32)
             )
         table_words = keep.tile([P, T], U32, name="table_words", align_bytes=64)
         nc.sync.dma_start(table_words[:].bitcast(I32), x_words[0].rearrange("p n t -> p (n t)").bitcast(I32))
-        two_t = load_list(two, "two_t")
-        offs_t = load_list(offs, "offs_t")
-        w3_raw = load_weight(w3, "w3_raw")
+        w3_raw = load_weight(w3, "w3_raw", 2)
         n4_t = load_list(n4, "n4_t")
         n3_t = load_list(n3, "n3_t")
-        w2_raw = load_weight(w2, "w2_raw")
+        w2_raw = load_weight(w2, "w2_raw", 1)
+        w1_raw = load_weight(w1, "w1_raw", 1)
         n2_t = load_list(n2, "n2_t")
-        w1_raw = load_weight(w1, "w1_raw")
         n1_t = load_list(n1, "n1_t")
         ga_t = keep.tile([P, PACK], F32, name="ga_t")
         nc.sync.dma_start(ga_t[:], ga.rearrange("(p t) o -> p (t o)", t=PACK))
@@ -82,13 +79,22 @@ def tile_picked_twktriebsendgwsum_none_p_kernel(
         warm = keep.tile([P, 1], F32, name="warm")
         nc.scalar.activation(warm[:], ident[:, 0:1], ACT.Sigmoid)
 
+        def windows(name):
+            return [
+                keep.tile([P, 2 * W], F32, name="%s%d" % (name, t), tag="%s%d" % (name, t), align_bytes=64)
+                for t in range(PACK)
+            ]
+
+        b_win, d_win, y_win, s_win = windows("b_win"), windows("d_win"), windows("y_win"), windows("s_win")
+        for t in range(PACK):
+            nc.gpsimd.memset(b_win[t][:, W:], 0.0)
+
         def pick_scales(offsets, name):
             picked = keep.tile([P, W], U8, name=name, align_bytes=64)
             nc.vector.tensor_copy(picked[:], table_scales[:].indirect(offsets[:]))
             return picked
 
-        def pick_words(offsets, name):
-            picked = keep.tile([P, W], U32, name=name, align_bytes=64)
+        def pick_words(offsets, picked):
             nc.vector.tensor_copy(picked[:], table_words[:].indirect(offsets[:]))
             return picked
 
@@ -98,12 +104,13 @@ def tile_picked_twktriebsendgwsum_none_p_kernel(
             nc.vector.quantize_mx(out=codes[:].bitcast(FP8X4), scales=scales[:], in_=grouped[:])
             return codes, scales
 
-        def group_weight(raw, name):
-            grouped = keep.tile([P, PACK * W], BF16, name=name + "_grouped", align_bytes=64)
-            nc.scalar.copy(
-                grouped[:].rearrange("p (t m j) -> p m j t", t=PACK, j=PACK),
-                raw[:].rearrange("p j (m t) -> p m j t", t=PACK),
-            )
+        def group_weight(parts, grouped):
+            dealt = grouped[:].rearrange("p (t m j) -> p m j t", t=PACK, j=PACK)
+            rows = P // len(parts)
+            for h, raw in enumerate(parts):
+                nc.scalar.copy(
+                    dealt[:, h * rows : (h + 1) * rows], raw[:].rearrange("p j (m t) -> p m j t", t=PACK)
+                )
             return grouped
 
         def product(acc, stationary, t, moving):
@@ -121,69 +128,75 @@ def tile_picked_twktriebsendgwsum_none_p_kernel(
         xs3 = pick_scales(three_t, "xs3")
         xs2 = pick_scales(two_t, "xs2")
         xs1 = pick_scales(offs_t, "xs1")
-        xw3 = pick_words(three_t, "xw3")
-        w3_q = quantize(group_weight(w3_raw, "w3"), "w3")
-        xw2 = pick_words(two_t, "xw2")
-        xw1 = pick_words(offs_t, "xw1")
+        xw3 = pick_words(three_t, keep.tile([P, W], U32, name="xw3", align_bytes=64))
+        xw2 = pick_words(two_t, keep.tile([P, W], U32, name="xw2", align_bytes=64))
+        w3_q = quantize(
+            group_weight(w3_raw, keep.tile([P, PACK * W], BF16, name="w3_grouped", tag="w3_grouped", align_bytes=64)), "w3"
+        )
+        xw1 = pick_words(offs_t, keep.tile([P, W], U32, name="xw1", tag="w3_grouped", align_bytes=64))
 
-        b_win, b_plain, b_sig, b_rise = [], [], [], []
+        b_plain = [d_win[t][:, W:] for t in range(PACK)]
+        b_rise = [y_win[t][:, W:] for t in range(PACK)]
+        last_sent = keep.tile([P, 2 * W], F32, name="last_sent", tag="last_sent")
+        b_plain[PACK - 1] = last_sent[:, 0:W]
+        b_rise[PACK - 1] = last_sent[:, W:]
+        nc.gpsimd.memset(d_win[PACK - 1][:, W:], 0.0)
+        nc.gpsimd.memset(y_win[PACK - 1][:, W:], 0.0)
+        b_diff = [s_win[t][:, W:] for t in range(PACK)]
+        b_banks = []
         for t in range(PACK):
             acc = bank(t)
             product(acc, w3_q, t, (xw3, xs3))
-            win = keep.tile([P, W], F32, name="b_win%d" % t)
-            nc.scalar.copy(win[:], acc[:])
-            plain = keep.tile([P, W], F32, name="b_plain%d" % t)
-            nc.scalar.copy(plain[:], acc[:])
+            nc.scalar.copy(b_win[t][:, 0:W], acc[:])
+            nc.scalar.copy(b_plain[t], acc[:])
+            nc.vector.tensor_tensor(b_diff[t], b_win[t][:].indirect(n4_t[:]), b_plain[t], ALU.subtract)
+            b_banks.append(acc)
+        for t in range(PACK):
+            nc.scalar.activation(b_rise[t], b_diff[t], ACT.Relu)
+        b_sig = []
+        for t in range(PACK):
             sig = keep.tile([P, W], F32, name="b_sig%d" % t)
-            nc.scalar.activation(sig[:], acc[:], ACT.Sigmoid)
-            diff = keep.tile([P, W], F32, name="b_diff%d" % t)
-            for cols, entries in halves(n4_t):
-                nc.vector.tensor_tensor(diff[:, cols], win[:].indirect(entries), plain[:, cols], ALU.subtract)
-            rise = keep.tile([P, W], F32, name="b_rise%d" % t)
-            nc.scalar.activation(rise[:], diff[:], ACT.Relu)
-            b_plain.append(plain)
-            b_sig.append(sig)
-            b_rise.append(rise)
+            nc.scalar.activation(sig[:], b_banks[t][:], ACT.Sigmoid)
+            weighted = keep.tile([P, W], F32, name="b_weighted%d" % t)
+            nc.scalar.activation(weighted[:], sig[:], ACT.Copy, scale=gb_t[:, t : t + 1])
+            b_sig.append(weighted)
 
-        w2_q = quantize(group_weight(w2_raw, "w2"), "w2")
-        d_win = []
+        w2_q = quantize(
+            group_weight(w2_raw, keep.tile([P, PACK * W], BF16, name="w2_grouped", tag="b_win0", align_bytes=64)), "w2"
+        )
         for t in range(PACK):
             acc = bank(4 + t)
             product(acc, w2_q, t, (xw2, xs2))
-            win = keep.tile([P, W], F32, name="d_win%d" % t)
-            nc.scalar.copy(win[:], acc[:])
-            d_win.append(win)
-        w1_q = quantize(group_weight(w1_raw, "w1"), "w1")
-        y_win = []
+            nc.scalar.copy(d_win[t][:, 0:W], acc[:])
+        w1_q = quantize(
+            group_weight(w1_raw, keep.tile([P, PACK * W], BF16, name="w1_grouped", tag="b_win1", align_bytes=64)), "w1"
+        )
         for t in range(PACK):
             acc = bank(t)
             product(acc, w1_q, t, (xw1, xs1))
-            win = keep.tile([P, W], F32, name="y_win%d" % t)
-            nc.scalar.activation(win[:], acc[:], ACT.Copy, scale=ga_t[:, t : t + 1])
-            y_win.append(win)
+            nc.scalar.activation(y_win[t][:, 0:W], acc[:], ACT.Copy, scale=ga_t[:, t : t + 1])
 
         def gather_and_turn(win, offsets, t, banks, name):
             fetched = keep.tile([P, W], F32, name=name)
-            for cols, entries in halves(offsets):
-                nc.vector.tensor_copy(fetched[:, cols], win[:].indirect(entries))
-            for jb in range(PACK):
-                cols = slice(jb * P, (jb + 1) * P)
-                dst = banks[jb][:, t * P : (t + 1) * P]
-                nc.tensor.matmul(dst, win[:, cols], ident[:], start=True, stop=False, is_transpose=True)
-                nc.tensor.matmul(dst, fetched[:, cols], ident[:], start=False, stop=True, is_transpose=True)
+            nc.vector.tensor_copy(fetched[:], win[:].indirect(offsets[:]))
+            for src, first in ((win, True), (fetched, False)):
+                for jb in range(PACK):
+                    dst = banks[jb][:, t * P : (t + 1) * P]
+                    nc.tensor.matmul(
+                        dst, src[:, jb * P : (jb + 1) * P], ident[:], start=first, stop=not first, is_transpose=True
+                    )
 
-        z2_planes = keep.tile([P, PACK, W], BF16, name="z2_planes")
+        z2_planes = keep.tile([P, PACK, W], BF16, name="z2_planes", tag="last_sent")
         d_banks = [bank(4 + jb) for jb in range(PACK)]
         y_banks = [bank(jb) for jb in range(PACK)]
         sent = []
         for t in range(PACK):
             ds = keep.tile([P, 2 * W], F32, name="ds%d" % t)
-            nc.vector.tensor_tensor(ds[:].indirect(n3_t[:]), b_rise[t][:], b_plain[t][:], ALU.add)
+            nc.vector.tensor_tensor(ds[:].indirect(n3_t[:]), b_rise[t], b_plain[t], ALU.add)
             sent.append(ds)
+        for t in range(PACK):
             gather_and_turn(d_win[t], n2_t, t, d_banks, "d_fetched%d" % t)
-            nc.vector.scalar_tensor_tensor(
-                z2_planes[:, t, :], ds[:, 0:W], gb_t[:, t : t + 1], b_sig[t][:], ALU.mult, ALU.mult
-            )
+            nc.gpsimd.tensor_tensor(z2_planes[:, t, :], sent[t][:, 0:W], b_sig[t][:], ALU.mult)
         z2_grouped = keep.tile([P, PACK * W], BF16, name="z2_grouped", align_bytes=64)
         nc.scalar.copy(
             z2_grouped[:].rearrange("p (c i t) -> p c t i", i=4, t=PACK),
@@ -231,22 +244,37 @@ def tile_picked_twktriebsendgwsum_none_p_kernel(
                 scales=z_scales[:, cols],
                 in_=z_grouped[:, t * W : (t + 1) * W],
             )
+        firsts, seconds = [], []
+
+        def finish(t, cols):
+            total = keep.tile([P, cols.stop - cols.start], F32, name="total%d_%d" % (t, cols.start))
+            nc.vector.tensor_tensor(total[:], firsts[t][:, cols], seconds[t][:, cols], ALU.add)
+            nc.sync.dma_start(out_rows[:, t, cols], total[:])
+
         for t in range(PACK):
             acc = bank(t)
             product(acc, (z_codes, z_scales), t, z2_q)
-            s_win = keep.tile([P, W], F32, name="s_win%d" % t)
-            nc.scalar.activation(s_win[:], acc[:], ACT.Copy, scale=0.0625)
+            if t == 0:
+                twin = bank(4)
+                product(twin, (z_codes, z_scales), t, z2_q)
+                nc.vector.tensor_scalar(s_win[t][:, 0:W], twin[:], 0.0625, None, ALU.mult)
+            else:
+                nc.scalar.activation(s_win[t][:, 0:W], acc[:], ACT.Copy, scale=0.0625)
             s_sig = keep.tile([P, W], F32, name="s_sig%d" % t)
             nc.scalar.activation(s_sig[:], acc[:], ACT.Sigmoid, scale=0.0625)
             s_sig7 = keep.tile([P, W], F32, name="s_sig7_%d" % t)
-            for cols, entries in halves(n7_t):
-                nc.scalar.activation(s_sig7[:, cols], s_win[:].indirect(entries), ACT.Sigmoid)
+            nc.scalar.activation(s_sig7[:], s_win[t][:].indirect(n7_t[:]), ACT.Sigmoid)
             first = keep.tile([P, W], F32, name="first%d" % t)
-            for cols, entries in halves(n5_t):
-                nc.vector.tensor_tensor(first[:, cols], s_win[:].indirect(entries), s_sig[:, cols], ALU.mult)
+            nc.vector.tensor_tensor(first[:], s_win[t][:].indirect(n5_t[:]), s_sig[:], ALU.mult)
+            firsts.append(first)
+            if t > 0:
+                finish(t - 1, slice(0, W))
             second = keep.tile([P, W], F32, name="second%d" % t)
-            for cols, entries in halves(n6_t):
-                nc.vector.tensor_tensor(second[:, cols], s_win[:].indirect(entries), s_sig7[:, cols], ALU.mult)
-            total = keep.tile([P, W], F32, name="total%d" % t)
-            nc.vector.tensor_tensor(total[:], first[:], second[:], ALU.add)
-            nc.sync.dma_start(out_rows[:, t, :], total[:])
+            seconds.append(second)
+            pieces = 2 if t == PACK - 1 else 1
+            for h in range(pieces):
+                cols = slice(h * W // pieces, (h + 1) * W // pieces)
+                entries = n6_t[:, h * LIST_COLS // pieces : (h + 1) * LIST_COLS // pieces]
+                nc.vector.tensor_tensor(second[:, cols], s_win[t][:].indirect(entries), s_sig7[:, cols], ALU.mult)
+        finish(PACK - 1, slice(0, W // 2))
+        finish(PACK - 1, slice(W // 2, W))

@@ -43,7 +43,7 @@ def tile_picked_twktriebsendgwsum_none_p_kernel(
             width = W // pieces
             parts = []
             for h in range(pieces):
-                raw = keep.tile([P, PACK, width], F32, name="%s%d" % (name, h))
+                raw = keep.tile([P, PACK, width], F32, name="%s%d" % (name, h), tag="%s%d" % (name, h))
                 nc.sync.dma_start(raw[:], src.rearrange("(p j) c -> p j c", j=PACK)[:, :, h * width : (h + 1) * width])
                 parts.append(raw)
             return parts
@@ -61,10 +61,10 @@ def tile_picked_twktriebsendgwsum_none_p_kernel(
         nc.sync.dma_start(table_words[:].bitcast(I32), x_words[0].rearrange("p n t -> p (n t)").bitcast(I32))
         w3_raw = load_weight(w3, "w3_raw", 2)
         n4_t = load_list(n4, "n4_t")
-        n3_t = load_list(n3, "n3_t")
-        w2_raw = load_weight(w2, "w2_raw", 1)
+        w2_raw = load_weight(w2, "w2_raw", 2)
         w1_raw = load_weight(w1, "w1_raw", 1)
         n2_t = load_list(n2, "n2_t")
+        n3_t = load_list(n3, "n3_t")
         n1_t = load_list(n1, "n1_t")
         ga_t = keep.tile([P, PACK], F32, name="ga_t")
         nc.sync.dma_start(ga_t[:], ga.rearrange("(p t) o -> p (t o)", t=PACK))
@@ -88,6 +88,7 @@ def tile_picked_twktriebsendgwsum_none_p_kernel(
         b_win, d_win, y_win, s_win = windows("b_win"), windows("d_win"), windows("y_win"), windows("s_win")
         for t in range(PACK):
             nc.gpsimd.memset(b_win[t][:, W:], 0.0)
+            nc.gpsimd.memset(y_win[t][:, W:], 0.0)
 
         def pick_scales(offsets, name):
             picked = keep.tile([P, W], U8, name=name, align_bytes=64)
@@ -113,14 +114,14 @@ def tile_picked_twktriebsendgwsum_none_p_kernel(
                 )
             return grouped
 
-        def product(acc, stationary, t, moving):
-            cols = slice(t * P, (t + 1) * P)
+        def product(acc, stationary, t, moving, cols=slice(0, W)):
+            rows = slice(t * P, (t + 1) * P)
             nc.tensor.matmul_mx(
-                out=acc[:],
-                lhsT=stationary[0][:, cols].bitcast(FP8X4),
-                lhsT_scale=stationary[1][:, cols],
-                rhs=moving[0][:].bitcast(FP8X4),
-                rhs_scale=moving[1][:],
+                out=acc[:, cols],
+                lhsT=stationary[0][:, rows].bitcast(FP8X4),
+                lhsT_scale=stationary[1][:, rows],
+                rhs=moving[0][:, cols].bitcast(FP8X4),
+                rhs_scale=moving[1][:, cols],
                 start=True,
                 stop=True,
             )
@@ -129,56 +130,52 @@ def tile_picked_twktriebsendgwsum_none_p_kernel(
         xs2 = pick_scales(two_t, "xs2")
         xs1 = pick_scales(offs_t, "xs1")
         xw3 = pick_words(three_t, keep.tile([P, W], U32, name="xw3", align_bytes=64))
-        xw2 = pick_words(two_t, keep.tile([P, W], U32, name="xw2", align_bytes=64))
+        xw2 = pick_words(two_t, keep.tile([P, W], U32, name="xw2", tag="xw2", align_bytes=64))
         w3_q = quantize(
             group_weight(w3_raw, keep.tile([P, PACK * W], BF16, name="w3_grouped", tag="w3_grouped", align_bytes=64)), "w3"
         )
         xw1 = pick_words(offs_t, keep.tile([P, W], U32, name="xw1", tag="w3_grouped", align_bytes=64))
 
-        b_plain = [d_win[t][:, W:] for t in range(PACK)]
-        b_rise = [y_win[t][:, W:] for t in range(PACK)]
-        last_sent = keep.tile([P, 2 * W], F32, name="last_sent", tag="last_sent")
-        b_plain[PACK - 1] = last_sent[:, 0:W]
-        b_rise[PACK - 1] = last_sent[:, W:]
-        nc.gpsimd.memset(d_win[PACK - 1][:, W:], 0.0)
-        nc.gpsimd.memset(y_win[PACK - 1][:, W:], 0.0)
+        b_fetched = [d_win[t][:, W:] for t in range(PACK)]
         b_diff = [s_win[t][:, W:] for t in range(PACK)]
-        b_banks = []
         for t in range(PACK):
             acc = bank(t)
             product(acc, w3_q, t, (xw3, xs3))
             nc.scalar.copy(b_win[t][:, 0:W], acc[:])
-            nc.scalar.copy(b_plain[t], acc[:])
-            nc.vector.tensor_tensor(b_diff[t], b_win[t][:].indirect(n4_t[:]), b_plain[t], ALU.subtract)
-            b_banks.append(acc)
+        w2_q = quantize(group_weight(w2_raw, keep.tile([P, PACK * W], BF16, name="w2_grouped", align_bytes=64)), "w2")
         for t in range(PACK):
-            nc.scalar.activation(b_rise[t], b_diff[t], ACT.Relu)
-        b_sig = []
-        for t in range(PACK):
-            sig = keep.tile([P, W], F32, name="b_sig%d" % t)
-            nc.scalar.activation(sig[:], b_banks[t][:], ACT.Sigmoid)
-            weighted = keep.tile([P, W], F32, name="b_weighted%d" % t)
-            nc.scalar.activation(weighted[:], sig[:], ACT.Copy, scale=gb_t[:, t : t + 1])
-            b_sig.append(weighted)
-
-        w2_q = quantize(
-            group_weight(w2_raw, keep.tile([P, PACK * W], BF16, name="w2_grouped", tag="b_win0", align_bytes=64)), "w2"
-        )
+            nc.vector.tensor_copy(b_fetched[t], b_win[t][:].indirect(n4_t[:]))
+            nc.gpsimd.tensor_tensor(b_diff[t], b_fetched[t], b_win[t][:, 0:W], ALU.subtract)
         for t in range(PACK):
             acc = bank(4 + t)
             product(acc, w2_q, t, (xw2, xs2))
             nc.scalar.copy(d_win[t][:, 0:W], acc[:])
         w1_q = quantize(
-            group_weight(w1_raw, keep.tile([P, PACK * W], BF16, name="w1_grouped", tag="b_win1", align_bytes=64)), "w1"
+            group_weight(w1_raw, keep.tile([P, PACK * W], BF16, name="w1_grouped", tag="xw2", align_bytes=64)), "w1"
         )
         for t in range(PACK):
             acc = bank(t)
             product(acc, w1_q, t, (xw1, xs1))
             nc.scalar.activation(y_win[t][:, 0:W], acc[:], ACT.Copy, scale=ga_t[:, t : t + 1])
 
-        def gather_and_turn(win, offsets, t, banks, name):
-            fetched = keep.tile([P, W], F32, name=name)
-            nc.vector.tensor_copy(fetched[:], win[:].indirect(offsets[:]))
+        rises = keep.tile([P, PACK, W], F32, name="rises", tag="w1_raw0")
+        b_rise = [rises[:, t, :] for t in range(PACK)]
+        b_sigs = keep.tile([P, PACK, W], F32, name="b_sigs", tag="w3_grouped", align_bytes=64)
+        b_sig = [b_sigs[:, t, :] for t in range(PACK)]
+        larger = []
+        for t in range(PACK):
+            nc.scalar.activation(b_rise[t], b_diff[t], ACT.Relu)
+            sm = keep.tile([P, W], F32, name="larger%d" % t, tag="larger%d" % t, align_bytes=64)
+            nc.gpsimd.tensor_tensor(sm[:], b_rise[t], b_win[t][:, 0:W], ALU.add)
+            larger.append(sm)
+
+        def send(t, tag):
+            ds = keep.tile([P, 2 * W], F32, name="ds%d" % t, tag=tag, align_bytes=64)
+            nc.vector.tensor_copy(ds[:].indirect(n3_t[:]), larger[t][:])
+            return ds
+
+        def gather_and_turn(win, offsets, t, banks, fetched):
+            nc.vector.tensor_copy(fetched, win[:].indirect(offsets[:]))
             for src, first in ((win, True), (fetched, False)):
                 for jb in range(PACK):
                     dst = banks[jb][:, t * P : (t + 1) * P]
@@ -186,25 +183,20 @@ def tile_picked_twktriebsendgwsum_none_p_kernel(
                         dst, src[:, jb * P : (jb + 1) * P], ident[:], start=first, stop=not first, is_transpose=True
                     )
 
-        z2_planes = keep.tile([P, PACK, W], BF16, name="z2_planes", tag="last_sent")
+        def weigh(t, tag):
+            weighted = keep.tile([P, W], F32, name="b_weighted%d" % t, tag=tag)
+            nc.scalar.activation(weighted[:], b_sig[t], ACT.Copy, scale=gb_t[:, t : t + 1])
+            return weighted
+
         d_banks = [bank(4 + jb) for jb in range(PACK)]
         y_banks = [bank(jb) for jb in range(PACK)]
-        sent = []
+        d_early = keep.tile([P, 2, W], F32, name="d_early")
+        d_late = keep.tile([P, 2, W], F32, name="d_late", tag="xw2", align_bytes=64)
         for t in range(PACK):
-            ds = keep.tile([P, 2 * W], F32, name="ds%d" % t)
-            nc.vector.tensor_tensor(ds[:].indirect(n3_t[:]), b_rise[t], b_plain[t], ALU.add)
-            sent.append(ds)
-        for t in range(PACK):
-            gather_and_turn(d_win[t], n2_t, t, d_banks, "d_fetched%d" % t)
-            nc.gpsimd.tensor_tensor(z2_planes[:, t, :], sent[t][:, 0:W], b_sig[t][:], ALU.mult)
-        z2_grouped = keep.tile([P, PACK * W], BF16, name="z2_grouped", align_bytes=64)
-        nc.scalar.copy(
-            z2_grouped[:].rearrange("p (c i t) -> p c t i", i=4, t=PACK),
-            z2_planes[:].rearrange("p t (c i) -> p c t i", i=4),
-        )
+            gather_and_turn(d_win[t], n2_t, t, d_banks, (d_early, d_late)[t // 2][:, t % 2, :])
         gates = []
         for jb in range(PACK):
-            gate = keep.tile([P, W], F32, name="gate%d" % jb)
+            gate = keep.tile([P, W], F32, name="gate%d" % jb, tag="gate%d" % jb)
             nc.scalar.activation(
                 gate[:].rearrange("j (u p e) -> j u p e", u=2, e=2),
                 d_banks[jb][:].rearrange("j (u e p) -> j u p e", u=2, e=2),
@@ -212,19 +204,22 @@ def tile_picked_twktriebsendgwsum_none_p_kernel(
             )
             gates.append(gate)
         for t in range(PACK):
-            gather_and_turn(y_win[t], n1_t, t, y_banks, "y_fetched%d" % t)
-        z2_q = quantize(z2_grouped, "z2")
+            fetched = keep.tile([P, W], F32, name="y_fetched%d" % t, tag="y_fetched%d" % t, align_bytes=64)
+            gather_and_turn(y_win[t], n1_t, t, y_banks, fetched[:])
+        for t in range(PACK):
+            nc.scalar.activation(b_sig[t], b_win[t][:, 0:W], ACT.Sigmoid)
+        sent = [send(0, "y_win2"), send(1, "y_win3"), send(2, "y_fetched3")]
 
         z_grouped = keep.tile([P, PACK * W], BF16, name="z_grouped", align_bytes=64)
         z_words = z_grouped[:].bitcast(F32).rearrange("p (t m u) -> p t m u", t=PACK, u=2)
         for jb in range(PACK):
-            z_turned = keep.tile([P, W], BF16, name="z_turned%d" % jb)
-            nc.vector.tensor_tensor(
-                z_turned[:].rearrange("j (u p e) -> j u p e", u=2, e=2),
+            summed = keep.tile([P, W], F32, name="summed%d" % jb, tag="summed%d" % jb, align_bytes=64)
+            nc.scalar.copy(
+                summed[:].rearrange("j (u p e) -> j u p e", u=2, e=2),
                 y_banks[jb][:].rearrange("j (u e p) -> j u p e", u=2, e=2),
-                gates[jb][:].rearrange("j (u p e) -> j u p e", u=2, e=2),
-                ALU.mult,
             )
+            z_turned = keep.tile([P, W], BF16, name="z_turned%d" % jb)
+            nc.gpsimd.tensor_tensor(z_turned[:], summed[:], gates[jb][:], ALU.mult)
             back = bank(4 + jb)
             pairs = z_turned[:].bitcast(F32)
             for u in range(2):
@@ -233,48 +228,84 @@ def tile_picked_twktriebsendgwsum_none_p_kernel(
                 z_words[:, :, 32 * jb : 32 * (jb + 1), :],
                 back[:, 0 : 2 * P].rearrange("p (u m t) -> p t m u", u=2, t=PACK),
             )
+        sent.append(send(3, "summed0"))
 
-        z_codes = keep.tile([P, W], U32, name="z_codes", align_bytes=64)
-        z_scales = keep.tile([P, W], U8, name="z_scales", align_bytes=64)
-        out_rows = out.rearrange("(p t) v -> p t v", t=PACK)
-        for t in range(PACK):
-            cols = slice(t * P, (t + 1) * P)
+        def quantize_z(first, count, tag):
+            name = "z%d" % first
+            codes = keep.tile([P, count * P], U32, name=name + "_codes", tag=tag, align_bytes=64)
+            scales = keep.tile([P, count * P], U8, name=name + "_scales", align_bytes=64)
             nc.vector.quantize_mx(
-                out=z_codes[:, cols].bitcast(FP8X4),
-                scales=z_scales[:, cols],
-                in_=z_grouped[:, t * W : (t + 1) * W],
+                out=codes[:].bitcast(FP8X4), scales=scales[:], in_=z_grouped[:, first * W : (first + count) * W]
             )
-        firsts, seconds = [], []
+            return codes, scales
 
-        def finish(t, cols):
-            total = keep.tile([P, cols.stop - cols.start], F32, name="total%d_%d" % (t, cols.start))
-            nc.vector.tensor_tensor(total[:], firsts[t][:, cols], seconds[t][:, cols], ALU.add)
-            nc.sync.dma_start(out_rows[:, t, cols], total[:])
+        z_first = quantize_z(0, 1, "z0_codes")
+        z2_planes = keep.tile([P, PACK, W], BF16, name="z2_planes", tag="z2_planes", align_bytes=64)
+        for t in range(PACK - 1):
+            nc.gpsimd.tensor_tensor(z2_planes[:, t, :], sent[t][:, 0:W], weigh(t, "gate%d" % (t + 1))[:], ALU.mult)
+        z2_grouped = keep.tile([P, PACK * W], BF16, name="z2_grouped", tag="z2_grouped", align_bytes=64)
+        z2_codes = keep.tile([P, W], U32, name="z2_codes", align_bytes=64)
+        z2_scales = keep.tile([P, W], U8, name="z2_scales", align_bytes=64)
+        halves = [slice(0, W // 2), slice(W // 2, W)]
+        for cols in halves:
+            nc.vector.scalar_tensor_tensor(
+                z2_planes[:, 3, cols], sent[3][:, cols], gb_t[:, 3:4], b_sigs[:, 3, cols], ALU.mult, ALU.mult
+            )
+        for cols, copy in zip(halves, (nc.scalar.copy, nc.vector.tensor_copy)):
+            copy(
+                z2_grouped[:, PACK * cols.start : PACK * cols.stop].rearrange("p (c i t) -> p c t i", i=4, t=PACK),
+                z2_planes[:, :, cols].rearrange("p t (c i) -> p c t i", i=4),
+            )
+        z2_q = (z2_codes, z2_scales)
+        s_banks = [bank(t) for t in range(PACK)]
+        twin = bank(4)
+        for cols in reversed(halves):
+            nc.vector.quantize_mx(
+                out=z2_codes[:, cols].bitcast(FP8X4),
+                scales=z2_scales[:, cols],
+                in_=z2_grouped[:, PACK * cols.start : PACK * cols.stop],
+            )
+            for acc in (twin, s_banks[0]):
+                product(acc, z_first, 0, z2_q, cols)
+        z_middle = quantize_z(1, 2, "z2_grouped")
+        z_last = quantize_z(3, 1, "z2_planes")
+        for t, (z_q, at) in enumerate(((z_middle, 0), (z_middle, 1), (z_last, 0)), start=1):
+            product(s_banks[t], z_q, at, z2_q)
 
-        for t in range(PACK):
-            acc = bank(t)
-            product(acc, (z_codes, z_scales), t, z2_q)
+        out_rows = out.rearrange("(p t) v -> p t v", t=PACK)
+        s_sig = [keep.tile([P, W], F32, name="s_sig%d" % t, tag="larger%d" % t, align_bytes=64) for t in range(PACK)]
+        far_sig = [keep.tile([P, W], F32, name="far_sig%d" % t) for t in range(PACK)]
+        firsts = [keep.tile([P, W], F32, name="first%d" % t) for t in range(PACK)]
+        seconds = [keep.tile([P, W], F32, name="second%d" % t) for t in range(PACK)]
+
+        def first_term(t):
             if t == 0:
-                twin = bank(4)
-                product(twin, (z_codes, z_scales), t, z2_q)
                 nc.vector.tensor_scalar(s_win[t][:, 0:W], twin[:], 0.0625, None, ALU.mult)
             else:
-                nc.scalar.activation(s_win[t][:, 0:W], acc[:], ACT.Copy, scale=0.0625)
-            s_sig = keep.tile([P, W], F32, name="s_sig%d" % t)
-            nc.scalar.activation(s_sig[:], acc[:], ACT.Sigmoid, scale=0.0625)
-            s_sig7 = keep.tile([P, W], F32, name="s_sig7_%d" % t)
-            nc.scalar.activation(s_sig7[:], s_win[t][:].indirect(n7_t[:]), ACT.Sigmoid)
-            first = keep.tile([P, W], F32, name="first%d" % t)
-            nc.vector.tensor_tensor(first[:], s_win[t][:].indirect(n5_t[:]), s_sig[:], ALU.mult)
-            firsts.append(first)
+                nc.scalar.activation(s_win[t][:, 0:W], s_banks[t][:], ACT.Copy, scale=0.0625)
+            nc.scalar.activation(s_sig[t][:], s_banks[t][:], ACT.Sigmoid, scale=0.0625)
+            nc.vector.tensor_tensor(firsts[t][:], s_win[t][:].indirect(n5_t[:]), s_sig[t][:], ALU.mult)
+
+        def second_term(t, pieces):
+            nc.scalar.activation(far_sig[t][:], s_win[t][:].indirect(n7_t[:]), ACT.Sigmoid)
+            for cols in pieces:
+                entries = n6_t[:, cols.start // 16 : cols.stop // 16]
+                nc.vector.tensor_tensor(
+                    seconds[t][:, cols], s_win[t][:].indirect(entries), far_sig[t][:, cols], ALU.mult
+                )
+
+        def finish(t, pieces):
+            for cols in pieces:
+                total = keep.tile([P, cols.stop - cols.start], F32, name="total%d_%d" % (t, cols.start))
+                nc.vector.tensor_tensor(total[:], firsts[t][:, cols], seconds[t][:, cols], ALU.add)
+                nc.sync.dma_start(out_rows[:, t, cols], total[:])
+
+        whole = [slice(0, W)]
+        first_term(0)
+        for t in range(PACK):
+            if t + 1 < PACK:
+                first_term(t + 1)
+            second_term(t, halves if t + 1 == PACK else whole)
             if t > 0:
-                finish(t - 1, slice(0, W))
-            second = keep.tile([P, W], F32, name="second%d" % t)
-            seconds.append(second)
-            pieces = 2 if t == PACK - 1 else 1
-            for h in range(pieces):
-                cols = slice(h * W // pieces, (h + 1) * W // pieces)
-                entries = n6_t[:, h * LIST_COLS // pieces : (h + 1) * LIST_COLS // pieces]
-                nc.vector.tensor_tensor(second[:, cols], s_win[t][:].indirect(entries), s_sig7[:, cols], ALU.mult)
-        finish(PACK - 1, slice(0, W // 2))
-        finish(PACK - 1, slice(W // 2, W))
+                finish(t - 1, whole)
+        finish(PACK - 1, halves)

@@ -76,8 +76,6 @@ def tile_picked_twktriebsendgwsum_none_p_kernel(
 
         ident = keep.tile([P, P], F32, name="ident")
         make_identity(nc, ident[:])
-        warm = keep.tile([P, 1], F32, name="warm")
-        nc.scalar.activation(warm[:], ident[:, 0:1], ACT.Sigmoid)
 
         def windows(name):
             return [
@@ -231,7 +229,7 @@ def tile_picked_twktriebsendgwsum_none_p_kernel(
         sent.append(send(3, "summed0"))
 
         def quantize_z(first, count, tag):
-            name = "z%d" % first
+            name = "z_rows%d" % first
             codes = keep.tile([P, count * P], U32, name=name + "_codes", tag=tag, align_bytes=64)
             scales = keep.tile([P, count * P], U8, name=name + "_scales", align_bytes=64)
             nc.vector.quantize_mx(
@@ -257,20 +255,20 @@ def tile_picked_twktriebsendgwsum_none_p_kernel(
                 z2_planes[:, :, cols].rearrange("p t (c i) -> p c t i", i=4),
             )
         z2_q = (z2_codes, z2_scales)
-        s_banks = [bank(t) for t in range(PACK)]
-        twin = bank(4)
-        for cols in reversed(halves):
+        copy_banks = [bank(4), bank(5)]
+        gate_banks = [bank(0), bank(6)]
+        for h in (1, 0):
+            cols = halves[h]
             nc.vector.quantize_mx(
                 out=z2_codes[:, cols].bitcast(FP8X4),
                 scales=z2_scales[:, cols],
                 in_=z2_grouped[:, PACK * cols.start : PACK * cols.stop],
             )
-            for acc in (twin, s_banks[0]):
+            for acc in (gate_banks[h], copy_banks[h]):
                 product(acc, z_first, 0, z2_q, cols)
-        z_middle = quantize_z(1, 2, "z2_grouped")
-        z_last = quantize_z(3, 1, "z2_planes")
-        for t, (z_q, at) in enumerate(((z_middle, 0), (z_middle, 1), (z_last, 0)), start=1):
-            product(s_banks[t], z_q, at, z2_q)
+        z_second = quantize_z(1, 1, "z2_planes")
+        s_banks = [None, bank(1), bank(2), bank(3)]
+        product(s_banks[1], z_second, 0, z2_q)
 
         out_rows = out.rearrange("(p t) v -> p t v", t=PACK)
         s_sig = [keep.tile([P, W], F32, name="s_sig%d" % t, tag="larger%d" % t, align_bytes=64) for t in range(PACK)]
@@ -280,32 +278,56 @@ def tile_picked_twktriebsendgwsum_none_p_kernel(
 
         def first_term(t):
             if t == 0:
-                nc.vector.tensor_scalar(s_win[t][:, 0:W], twin[:], 0.0625, None, ALU.mult)
+                for h in (1, 0):
+                    cols = halves[h]
+                    nc.vector.tensor_scalar(s_win[t][:, cols], copy_banks[h][:, cols], 0.0625, None, ALU.mult)
+                    nc.scalar.activation(s_sig[t][:, cols], gate_banks[h][:, cols], ACT.Sigmoid, scale=0.0625)
             else:
                 nc.scalar.activation(s_win[t][:, 0:W], s_banks[t][:], ACT.Copy, scale=0.0625)
-            nc.scalar.activation(s_sig[t][:], s_banks[t][:], ACT.Sigmoid, scale=0.0625)
+                nc.scalar.activation(s_sig[t][:], s_banks[t][:], ACT.Sigmoid, scale=0.0625)
             nc.vector.tensor_tensor(firsts[t][:], s_win[t][:].indirect(n5_t[:]), s_sig[t][:], ALU.mult)
 
-        def second_term(t, pieces):
-            nc.scalar.activation(far_sig[t][:], s_win[t][:].indirect(n7_t[:]), ACT.Sigmoid)
-            for cols in pieces:
-                entries = n6_t[:, cols.start // 16 : cols.stop // 16]
-                nc.vector.tensor_tensor(
-                    seconds[t][:, cols], s_win[t][:].indirect(entries), far_sig[t][:, cols], ALU.mult
-                )
+        def second_term(t, cols):
+            entries = n6_t[:, cols.start // 16 : cols.stop // 16]
+            nc.vector.tensor_tensor(seconds[t][:, cols], s_win[t][:].indirect(entries), far_sig[t][:, cols], ALU.mult)
 
-        def finish(t, pieces):
-            for cols in pieces:
-                total = keep.tile([P, cols.stop - cols.start], F32, name="total%d_%d" % (t, cols.start))
-                nc.vector.tensor_tensor(total[:], firsts[t][:, cols], seconds[t][:, cols], ALU.add)
-                nc.sync.dma_start(out_rows[:, t, cols], total[:])
+        def finish(t, cols):
+            total = keep.tile([P, cols.stop - cols.start], F32, name="total%d_%d" % (t, cols.start))
+            nc.vector.tensor_tensor(total[:], firsts[t][:, cols], seconds[t][:, cols], ALU.add)
+            nc.sync.dma_start(out_rows[:, t, cols], total[:])
 
-        whole = [slice(0, W)]
+        def finish_turned(t):
+            there, back = bank(4 + 2 * (t % 2)), bank(5 + 2 * (t % 2))
+            for vb in range(PACK):
+                cols = slice(vb * P, (vb + 1) * P)
+                for src, first in ((firsts[t], True), (seconds[t], False)):
+                    nc.tensor.matmul(
+                        there[:, cols], src[:, cols], ident[:], start=first, stop=not first, is_transpose=True
+                    )
+            turned = keep.tile([P, W], F32, name="turned%d" % t, tag="summed%d" % (t + 1), align_bytes=64)
+            nc.scalar.copy(turned[:], there[:])
+            for vb in range(PACK):
+                cols = slice(vb * P, (vb + 1) * P)
+                nc.tensor.transpose(back[:, cols], turned[:, cols], ident[:])
+            total = keep.tile([P, W], F32, name="total%d" % t)
+            nc.scalar.copy(total[:], back[:])
+            nc.sync.dma_start(out_rows[:, t, :], total[:])
+
+        whole = slice(0, W)
         first_term(0)
+        z_rest = quantize_z(2, 2, "z2_grouped")
+        for t in (2, 3):
+            product(s_banks[t], z_rest, t - 2, z2_q)
+        ending = [slice(0, 3 * W // 4), slice(3 * W // 4, W)]
         for t in range(PACK):
             if t + 1 < PACK:
                 first_term(t + 1)
-            second_term(t, halves if t + 1 == PACK else whole)
-            if t > 0:
+            nc.scalar.activation(far_sig[t][:], s_win[t][:].indirect(n7_t[:]), ACT.Sigmoid)
+            second_term(t, whole if t + 1 < PACK else ending[0])
+            if t == 2:
+                finish_turned(0)
+            if t > 1:
                 finish(t - 1, whole)
-        finish(PACK - 1, halves)
+        second_term(PACK - 1, ending[1])
+        for cols in ending:
+            finish(PACK - 1, cols)

@@ -17,7 +17,10 @@ P = 128
 PACK = 4
 T = 2048
 W = 512
-LIST_COLS = W // 16
+GROUP = 16
+QUADRANT = 32
+S_FACTOR = 0.0625
+LAST = PACK - 1
 
 FLOPS = 4 * 2 * 512 * 512 * 512
 
@@ -34,8 +37,11 @@ def tile_picked_twktriebsendgwsum_none_p_kernel(
         def bank(i):
             return psum.tile([P, W], F32, name="bank%d" % i, tag="bank%d" % i)
 
+        def block(i):
+            return slice(i * P, (i + 1) * P)
+
         def load_list(src, name):
-            tile = lists.tile([P, LIST_COLS], U16, name=name)
+            tile = lists.tile([P, W // GROUP], U16, name=name)
             nc.sync.dma_start(tile[:], src)
             return tile
 
@@ -53,9 +59,10 @@ def tile_picked_twktriebsendgwsum_none_p_kernel(
         three_t = load_list(three, "three_t")
         two_t = load_list(two, "two_t")
         offs_t = load_list(offs, "offs_t")
-        for q in range(4):
+        for q in range(P // QUADRANT):
             nc.sync.dma_start(
-                table_scales[32 * q : 32 * q + 4, :].bitcast(I32), x_scales[0, 4 * q : 4 * q + 4, :].bitcast(I32)
+                table_scales[QUADRANT * q : QUADRANT * q + 4, :].bitcast(I32),
+                x_scales[0, 4 * q : 4 * q + 4, :].bitcast(I32),
             )
         table_words = keep.tile([P, T], U32, name="table_words", align_bytes=64)
         nc.sync.dma_start(table_words[:].bitcast(I32), x_words[0].rearrange("p n t -> p (n t)").bitcast(I32))
@@ -76,6 +83,8 @@ def tile_picked_twktriebsendgwsum_none_p_kernel(
 
         ident = keep.tile([P, P], F32, name="ident")
         make_identity(nc, ident[:])
+        warm = keep.tile([P, 1], F32, name="warm")
+        nc.scalar.activation(warm[:], ident[:, 0:1], ACT.Sigmoid)
 
         def windows(name):
             return [
@@ -87,146 +96,128 @@ def tile_picked_twktriebsendgwsum_none_p_kernel(
         for t in range(PACK):
             nc.gpsimd.memset(b_win[t][:, W:], 0.0)
             nc.gpsimd.memset(y_win[t][:, W:], 0.0)
+        b_fetched = [d_win[t][:, W:] for t in range(PACK)]
+        b_diff = [s_win[t][:, W:] for t in range(PACK)]
 
         def pick_scales(offsets, name):
             picked = keep.tile([P, W], U8, name=name, align_bytes=64)
             nc.vector.tensor_copy(picked[:], table_scales[:].indirect(offsets[:]))
             return picked
 
-        def pick_words(offsets, picked):
+        def pick_words(offsets, name, tag):
+            picked = keep.tile([P, W], U32, name=name, tag=tag, align_bytes=64)
             nc.vector.tensor_copy(picked[:], table_words[:].indirect(offsets[:]))
             return picked
 
-        def quantize(grouped, name):
+        def quantize_weight(parts, name, tag):
+            grouped = keep.tile([P, PACK * W], BF16, name=name + "_grouped", tag=tag, align_bytes=64)
+            dealt = grouped[:].rearrange("p (t m j) -> p m j t", t=PACK, j=PACK)
+            rows = P // len(parts)
+            for h, raw in enumerate(parts):
+                nc.scalar.copy(dealt[:, h * rows : (h + 1) * rows], raw[:].rearrange("p j (m t) -> p m j t", t=PACK))
             codes = keep.tile([P, W], U32, name=name + "_codes", align_bytes=64)
             scales = keep.tile([P, W], U8, name=name + "_scales", align_bytes=64)
             nc.vector.quantize_mx(out=codes[:].bitcast(FP8X4), scales=scales[:], in_=grouped[:])
             return codes, scales
 
-        def group_weight(parts, grouped):
-            dealt = grouped[:].rearrange("p (t m j) -> p m j t", t=PACK, j=PACK)
-            rows = P // len(parts)
-            for h, raw in enumerate(parts):
-                nc.scalar.copy(
-                    dealt[:, h * rows : (h + 1) * rows], raw[:].rearrange("p j (m t) -> p m j t", t=PACK)
-                )
-            return grouped
-
-        def product(acc, stationary, t, moving, cols=slice(0, W)):
-            rows = slice(t * P, (t + 1) * P)
+        def product(acc, stationary, at, moving, cols=slice(0, W)):
             nc.tensor.matmul_mx(
                 out=acc[:, cols],
-                lhsT=stationary[0][:, rows].bitcast(FP8X4),
-                lhsT_scale=stationary[1][:, rows],
+                lhsT=stationary[0][:, block(at)].bitcast(FP8X4),
+                lhsT_scale=stationary[1][:, block(at)],
                 rhs=moving[0][:, cols].bitcast(FP8X4),
                 rhs_scale=moving[1][:, cols],
                 start=True,
                 stop=True,
             )
 
-        xs3 = pick_scales(three_t, "xs3")
-        xs2 = pick_scales(two_t, "xs2")
-        xs1 = pick_scales(offs_t, "xs1")
-        xw3 = pick_words(three_t, keep.tile([P, W], U32, name="xw3", align_bytes=64))
-        xw2 = pick_words(two_t, keep.tile([P, W], U32, name="xw2", tag="xw2", align_bytes=64))
-        w3_q = quantize(
-            group_weight(w3_raw, keep.tile([P, PACK * W], BF16, name="w3_grouped", tag="w3_grouped", align_bytes=64)), "w3"
-        )
-        xw1 = pick_words(offs_t, keep.tile([P, W], U32, name="xw1", tag="w3_grouped", align_bytes=64))
+        three_scales = pick_scales(three_t, "three_scales")
+        two_scales = pick_scales(two_t, "two_scales")
+        offs_scales = pick_scales(offs_t, "offs_scales")
+        three_words = pick_words(three_t, "three_words", "three_words")
+        two_words = pick_words(two_t, "two_words", "two_words")
+        w3_q = quantize_weight(w3_raw, "w3", "w3_grouped")
+        offs_words = pick_words(offs_t, "offs_words", "w3_grouped")
 
-        b_fetched = [d_win[t][:, W:] for t in range(PACK)]
-        b_diff = [s_win[t][:, W:] for t in range(PACK)]
         for t in range(PACK):
             acc = bank(t)
-            product(acc, w3_q, t, (xw3, xs3))
+            product(acc, w3_q, t, (three_words, three_scales))
             nc.scalar.copy(b_win[t][:, 0:W], acc[:])
-        w2_q = quantize(group_weight(w2_raw, keep.tile([P, PACK * W], BF16, name="w2_grouped", align_bytes=64)), "w2")
+        w2_q = quantize_weight(w2_raw, "w2", "w2_grouped")
         for t in range(PACK):
             nc.vector.tensor_copy(b_fetched[t], b_win[t][:].indirect(n4_t[:]))
             nc.gpsimd.tensor_tensor(b_diff[t], b_fetched[t], b_win[t][:, 0:W], ALU.subtract)
         for t in range(PACK):
-            acc = bank(4 + t)
-            product(acc, w2_q, t, (xw2, xs2))
+            acc = bank(PACK + t)
+            product(acc, w2_q, t, (two_words, two_scales))
             nc.scalar.copy(d_win[t][:, 0:W], acc[:])
-        w1_q = quantize(
-            group_weight(w1_raw, keep.tile([P, PACK * W], BF16, name="w1_grouped", tag="xw2", align_bytes=64)), "w1"
-        )
+        w1_q = quantize_weight(w1_raw, "w1", "two_words")
         for t in range(PACK):
             acc = bank(t)
-            product(acc, w1_q, t, (xw1, xs1))
+            product(acc, w1_q, t, (offs_words, offs_scales))
             nc.scalar.activation(y_win[t][:, 0:W], acc[:], ACT.Copy, scale=ga_t[:, t : t + 1])
 
-        rises = keep.tile([P, PACK, W], F32, name="rises", tag="w1_raw0")
-        b_rise = [rises[:, t, :] for t in range(PACK)]
-        b_sigs = keep.tile([P, PACK, W], F32, name="b_sigs", tag="w3_grouped", align_bytes=64)
-        b_sig = [b_sigs[:, t, :] for t in range(PACK)]
-        larger = []
+        b_rise = keep.tile([P, PACK, W], F32, name="b_rise", tag="w1_raw0")
+        b_sig = keep.tile([P, PACK, W], F32, name="b_sig", tag="w3_grouped", align_bytes=64)
+        sm = []
         for t in range(PACK):
-            nc.scalar.activation(b_rise[t], b_diff[t], ACT.Relu)
-            sm = keep.tile([P, W], F32, name="larger%d" % t, tag="larger%d" % t, align_bytes=64)
-            nc.gpsimd.tensor_tensor(sm[:], b_rise[t], b_win[t][:, 0:W], ALU.add)
-            larger.append(sm)
+            nc.scalar.activation(b_rise[:, t, :], b_diff[t], ACT.Relu)
+            sm.append(keep.tile([P, W], F32, name="sm%d" % t, tag="sm%d" % t, align_bytes=64))
+            nc.gpsimd.tensor_tensor(sm[t][:], b_rise[:, t, :], b_win[t][:, 0:W], ALU.add)
 
-        def send(t, tag):
-            ds = keep.tile([P, 2 * W], F32, name="ds%d" % t, tag=tag, align_bytes=64)
-            nc.vector.tensor_copy(ds[:].indirect(n3_t[:]), larger[t][:])
-            return ds
+        def scatter_sm(t, tag):
+            window = keep.tile([P, 2 * W], F32, name="ds%d" % t, tag=tag, align_bytes=64)
+            nc.vector.tensor_copy(window[:].indirect(n3_t[:]), sm[t][:])
+            return window
 
-        def gather_and_turn(win, offsets, t, banks, fetched):
+        def gather_and_add_turned(win, offsets, t, banks, fetched):
             nc.vector.tensor_copy(fetched, win[:].indirect(offsets[:]))
             for src, first in ((win, True), (fetched, False)):
-                for jb in range(PACK):
-                    dst = banks[jb][:, t * P : (t + 1) * P]
+                for c in range(PACK):
                     nc.tensor.matmul(
-                        dst, src[:, jb * P : (jb + 1) * P], ident[:], start=first, stop=not first, is_transpose=True
+                        banks[c][:, block(t)], src[:, block(c)], ident[:], start=first, stop=not first, is_transpose=True
                     )
 
-        def weigh(t, tag):
-            weighted = keep.tile([P, W], F32, name="b_weighted%d" % t, tag=tag)
-            nc.scalar.activation(weighted[:], b_sig[t], ACT.Copy, scale=gb_t[:, t : t + 1])
-            return weighted
+        def in_word_order(tile):
+            return tile[:].rearrange("j (u p e) -> j u p e", u=2, e=2)
 
-        d_banks = [bank(4 + jb) for jb in range(PACK)]
-        y_banks = [bank(jb) for jb in range(PACK)]
+        def from_tile_order(tile):
+            return tile[:].rearrange("j (u e p) -> j u p e", u=2, e=2)
+
+        d_banks = [bank(PACK + c) for c in range(PACK)]
+        y_banks = [bank(c) for c in range(PACK)]
         d_early = keep.tile([P, 2, W], F32, name="d_early")
-        d_late = keep.tile([P, 2, W], F32, name="d_late", tag="xw2", align_bytes=64)
+        d_late = keep.tile([P, 2, W], F32, name="d_late", tag="two_words", align_bytes=64)
         for t in range(PACK):
-            gather_and_turn(d_win[t], n2_t, t, d_banks, (d_early, d_late)[t // 2][:, t % 2, :])
-        gates = []
-        for jb in range(PACK):
-            gate = keep.tile([P, W], F32, name="gate%d" % jb, tag="gate%d" % jb)
-            nc.scalar.activation(
-                gate[:].rearrange("j (u p e) -> j u p e", u=2, e=2),
-                d_banks[jb][:].rearrange("j (u e p) -> j u p e", u=2, e=2),
-                ACT.Sigmoid,
-            )
-            gates.append(gate)
+            gather_and_add_turned(d_win[t], n2_t, t, d_banks, (d_early, d_late)[t // 2][:, t % 2, :])
+        d_gate = []
+        for c in range(PACK):
+            d_gate.append(keep.tile([P, W], F32, name="d_gate%d" % c, tag="d_gate%d" % c))
+            nc.scalar.activation(in_word_order(d_gate[c]), from_tile_order(d_banks[c]), ACT.Sigmoid)
         for t in range(PACK):
             fetched = keep.tile([P, W], F32, name="y_fetched%d" % t, tag="y_fetched%d" % t, align_bytes=64)
-            gather_and_turn(y_win[t], n1_t, t, y_banks, fetched[:])
+            gather_and_add_turned(y_win[t], n1_t, t, y_banks, fetched[:])
         for t in range(PACK):
-            nc.scalar.activation(b_sig[t], b_win[t][:, 0:W], ACT.Sigmoid)
-        sent = [send(0, "y_win2"), send(1, "y_win3"), send(2, "y_fetched3")]
+            nc.scalar.activation(b_sig[:, t, :], b_win[t][:, 0:W], ACT.Sigmoid)
+        ds = [scatter_sm(0, "y_win2"), scatter_sm(1, "y_win3"), scatter_sm(2, "y_fetched3")]
 
         z_grouped = keep.tile([P, PACK * W], BF16, name="z_grouped", align_bytes=64)
         z_words = z_grouped[:].bitcast(F32).rearrange("p (t m u) -> p t m u", t=PACK, u=2)
-        for jb in range(PACK):
-            summed = keep.tile([P, W], F32, name="summed%d" % jb, tag="summed%d" % jb, align_bytes=64)
-            nc.scalar.copy(
-                summed[:].rearrange("j (u p e) -> j u p e", u=2, e=2),
-                y_banks[jb][:].rearrange("j (u e p) -> j u p e", u=2, e=2),
-            )
-            z_turned = keep.tile([P, W], BF16, name="z_turned%d" % jb)
-            nc.gpsimd.tensor_tensor(z_turned[:], summed[:], gates[jb][:], ALU.mult)
-            back = bank(4 + jb)
+        per_block = P // PACK
+        for c in range(PACK):
+            y_sum = keep.tile([P, W], F32, name="y_sum%d" % c, tag="y_sum%d" % c, align_bytes=64)
+            nc.scalar.copy(in_word_order(y_sum), from_tile_order(y_banks[c]))
+            z_turned = keep.tile([P, W], BF16, name="z_turned%d" % c)
+            nc.gpsimd.tensor_tensor(z_turned[:], y_sum[:], d_gate[c][:], ALU.mult)
+            back = bank(PACK + c)
             pairs = z_turned[:].bitcast(F32)
             for u in range(2):
-                nc.tensor.transpose(back[:, u * P : (u + 1) * P], pairs[:, u * P : (u + 1) * P], ident[:])
+                nc.tensor.transpose(back[:, block(u)], pairs[:, block(u)], ident[:])
             nc.scalar.copy(
-                z_words[:, :, 32 * jb : 32 * (jb + 1), :],
+                z_words[:, :, per_block * c : per_block * (c + 1), :],
                 back[:, 0 : 2 * P].rearrange("p (u m t) -> p t m u", u=2, t=PACK),
             )
-        sent.append(send(3, "summed0"))
+        ds.append(scatter_sm(LAST, "y_sum0"))
 
         def quantize_z(first, count, tag):
             name = "z_rows%d" % first
@@ -237,26 +228,30 @@ def tile_picked_twktriebsendgwsum_none_p_kernel(
             )
             return codes, scales
 
-        z_first = quantize_z(0, 1, "z0_codes")
-        z2_planes = keep.tile([P, PACK, W], BF16, name="z2_planes", tag="z2_planes", align_bytes=64)
-        for t in range(PACK - 1):
-            nc.gpsimd.tensor_tensor(z2_planes[:, t, :], sent[t][:, 0:W], weigh(t, "gate%d" % (t + 1))[:], ALU.mult)
+        z_first = quantize_z(0, 1, "z_first")
+
+        z2_tiles = keep.tile([P, PACK, W], BF16, name="z2_tiles", tag="z2_tiles", align_bytes=64)
+        for t in range(LAST):
+            weighted = keep.tile([P, W], F32, name="b_weighted%d" % t, tag="d_gate%d" % (t + 1))
+            nc.scalar.activation(weighted[:], b_sig[:, t, :], ACT.Copy, scale=gb_t[:, t : t + 1])
+            nc.gpsimd.tensor_tensor(z2_tiles[:, t, :], ds[t][:, 0:W], weighted[:], ALU.mult)
         z2_grouped = keep.tile([P, PACK * W], BF16, name="z2_grouped", tag="z2_grouped", align_bytes=64)
         z2_codes = keep.tile([P, W], U32, name="z2_codes", align_bytes=64)
         z2_scales = keep.tile([P, W], U8, name="z2_scales", align_bytes=64)
+        z2_q = (z2_codes, z2_scales)
         halves = [slice(0, W // 2), slice(W // 2, W)]
         for cols in halves:
             nc.vector.scalar_tensor_tensor(
-                z2_planes[:, 3, cols], sent[3][:, cols], gb_t[:, 3:4], b_sigs[:, 3, cols], ALU.mult, ALU.mult
+                z2_tiles[:, LAST, cols], ds[LAST][:, cols], gb_t[:, LAST:PACK], b_sig[:, LAST, cols], ALU.mult, ALU.mult
             )
         for cols, copy in zip(halves, (nc.scalar.copy, nc.vector.tensor_copy)):
             copy(
                 z2_grouped[:, PACK * cols.start : PACK * cols.stop].rearrange("p (c i t) -> p c t i", i=4, t=PACK),
-                z2_planes[:, :, cols].rearrange("p t (c i) -> p c t i", i=4),
+                z2_tiles[:, :, cols].rearrange("p t (c i) -> p c t i", i=4),
             )
-        z2_q = (z2_codes, z2_scales)
+
         copy_banks = [bank(4), bank(5)]
-        gate_banks = [bank(0), bank(6)]
+        sigmoid_banks = [bank(0), bank(6)]
         for h in (1, 0):
             cols = halves[h]
             nc.vector.quantize_mx(
@@ -264,14 +259,14 @@ def tile_picked_twktriebsendgwsum_none_p_kernel(
                 scales=z2_scales[:, cols],
                 in_=z2_grouped[:, PACK * cols.start : PACK * cols.stop],
             )
-            for acc in (gate_banks[h], copy_banks[h]):
+            for acc in (sigmoid_banks[h], copy_banks[h]):
                 product(acc, z_first, 0, z2_q, cols)
-        z_second = quantize_z(1, 1, "z2_planes")
-        s_banks = [None, bank(1), bank(2), bank(3)]
+        z_second = quantize_z(1, 1, "z2_tiles")
+        s_banks = {t: bank(t) for t in range(1, PACK)}
         product(s_banks[1], z_second, 0, z2_q)
 
         out_rows = out.rearrange("(p t) v -> p t v", t=PACK)
-        s_sig = [keep.tile([P, W], F32, name="s_sig%d" % t, tag="larger%d" % t, align_bytes=64) for t in range(PACK)]
+        s_sig = [keep.tile([P, W], F32, name="s_sig%d" % t, tag="sm%d" % t, align_bytes=64) for t in range(PACK)]
         far_sig = [keep.tile([P, W], F32, name="far_sig%d" % t) for t in range(PACK)]
         firsts = [keep.tile([P, W], F32, name="first%d" % t) for t in range(PACK)]
         seconds = [keep.tile([P, W], F32, name="second%d" % t) for t in range(PACK)]
@@ -280,54 +275,52 @@ def tile_picked_twktriebsendgwsum_none_p_kernel(
             if t == 0:
                 for h in (1, 0):
                     cols = halves[h]
-                    nc.vector.tensor_scalar(s_win[t][:, cols], copy_banks[h][:, cols], 0.0625, None, ALU.mult)
-                    nc.scalar.activation(s_sig[t][:, cols], gate_banks[h][:, cols], ACT.Sigmoid, scale=0.0625)
+                    nc.vector.tensor_scalar(s_win[t][:, cols], copy_banks[h][:, cols], S_FACTOR, None, ALU.mult)
+                    nc.scalar.activation(s_sig[t][:, cols], sigmoid_banks[h][:, cols], ACT.Sigmoid, scale=S_FACTOR)
             else:
-                nc.scalar.activation(s_win[t][:, 0:W], s_banks[t][:], ACT.Copy, scale=0.0625)
-                nc.scalar.activation(s_sig[t][:], s_banks[t][:], ACT.Sigmoid, scale=0.0625)
+                nc.scalar.activation(s_win[t][:, 0:W], s_banks[t][:], ACT.Copy, scale=S_FACTOR)
+                nc.scalar.activation(s_sig[t][:], s_banks[t][:], ACT.Sigmoid, scale=S_FACTOR)
             nc.vector.tensor_tensor(firsts[t][:], s_win[t][:].indirect(n5_t[:]), s_sig[t][:], ALU.mult)
 
         def second_term(t, cols):
-            entries = n6_t[:, cols.start // 16 : cols.stop // 16]
+            entries = n6_t[:, cols.start // GROUP : cols.stop // GROUP]
             nc.vector.tensor_tensor(seconds[t][:, cols], s_win[t][:].indirect(entries), far_sig[t][:, cols], ALU.mult)
 
-        def finish(t, cols):
+        def add_and_store(t, cols):
             total = keep.tile([P, cols.stop - cols.start], F32, name="total%d_%d" % (t, cols.start))
             nc.vector.tensor_tensor(total[:], firsts[t][:, cols], seconds[t][:, cols], ALU.add)
             nc.sync.dma_start(out_rows[:, t, cols], total[:])
 
-        def finish_turned(t):
-            there, back = bank(4 + 2 * (t % 2)), bank(5 + 2 * (t % 2))
-            for vb in range(PACK):
-                cols = slice(vb * P, (vb + 1) * P)
+        def add_turned_and_store(t):
+            there, back = bank(4), bank(5)
+            for c in range(PACK):
                 for src, first in ((firsts[t], True), (seconds[t], False)):
                     nc.tensor.matmul(
-                        there[:, cols], src[:, cols], ident[:], start=first, stop=not first, is_transpose=True
+                        there[:, block(c)], src[:, block(c)], ident[:], start=first, stop=not first, is_transpose=True
                     )
-            turned = keep.tile([P, W], F32, name="turned%d" % t, tag="summed%d" % (t + 1), align_bytes=64)
+            turned = keep.tile([P, W], F32, name="turned", tag="y_sum1", align_bytes=64)
             nc.scalar.copy(turned[:], there[:])
-            for vb in range(PACK):
-                cols = slice(vb * P, (vb + 1) * P)
-                nc.tensor.transpose(back[:, cols], turned[:, cols], ident[:])
-            total = keep.tile([P, W], F32, name="total%d" % t)
+            for c in range(PACK):
+                nc.tensor.transpose(back[:, block(c)], turned[:, block(c)], ident[:])
+            total = keep.tile([P, W], F32, name="total_turned")
             nc.scalar.copy(total[:], back[:])
             nc.sync.dma_start(out_rows[:, t, :], total[:])
 
-        whole = slice(0, W)
         first_term(0)
         z_rest = quantize_z(2, 2, "z2_grouped")
         for t in (2, 3):
             product(s_banks[t], z_rest, t - 2, z2_q)
+        whole = slice(0, W)
         ending = [slice(0, 3 * W // 4), slice(3 * W // 4, W)]
         for t in range(PACK):
-            if t + 1 < PACK:
+            if t < LAST:
                 first_term(t + 1)
             nc.scalar.activation(far_sig[t][:], s_win[t][:].indirect(n7_t[:]), ACT.Sigmoid)
-            second_term(t, whole if t + 1 < PACK else ending[0])
-            if t == 2:
-                finish_turned(0)
+            second_term(t, whole if t < LAST else ending[0])
+            if t == LAST - 1:
+                add_turned_and_store(0)
             if t > 1:
-                finish(t - 1, whole)
-        second_term(PACK - 1, ending[1])
+                add_and_store(t - 1, whole)
+        second_term(LAST, ending[1])
         for cols in ending:
-            finish(PACK - 1, cols)
+            add_and_store(LAST, cols)

from contextlib import ExitStack

import concourse.mybir as mybir
from concourse.masks import make_identity

F32 = mybir.dt.float32
BF16 = mybir.dt.bfloat16
I32 = mybir.dt.int32
U32 = mybir.dt.uint32
U16 = mybir.dt.uint16
U8 = mybir.dt.uint8
FP8X4 = mybir.dt.float8_e4m3fn_x4
ACT = mybir.ActivationFunctionType
ALU = mybir.AluOpType

P = 128
PACK = 4
T = 2048
W = 512
GROUP = 16
QUADRANT = 32
S_FACTOR = 0.0625
LAST = PACK - 1

FLOPS = 4 * 2 * 512 * 512 * 512


def tile_picked_twktriebsendgwsum_none_p_kernel(
    tc, x_words, x_scales, w1, w2, w3, ga, gb, offs, two, n1, n2, three, n3, n4, n5, n6, n7, out
):
    nc = tc.nc
    with ExitStack() as ctx:
        lists = ctx.enter_context(tc.tile_pool(name="lists", bufs=1))
        keep = ctx.enter_context(tc.tile_pool(name="keep", bufs=1))
        psum = ctx.enter_context(tc.psum_pool(name="psum", bufs=1))

        def bank(i):
            return psum.tile([P, W], F32, name="bank%d" % i, tag="bank%d" % i)

        def block(i):
            return slice(i * P, (i + 1) * P)

        def load_list(src, name):
            tile = lists.tile([P, W // GROUP], U16, name=name)
            nc.sync.dma_start(tile[:], src)
            return tile

        def load_weight(src, name, pieces):
            width = W // pieces
            parts = []
            for h in range(pieces):
                raw = keep.tile([P, PACK, width], F32, name="%s%d" % (name, h), tag="%s%d" % (name, h))
                nc.sync.dma_start(raw[:], src.rearrange("(p j) c -> p j c", j=PACK)[:, :, h * width : (h + 1) * width])
                parts.append(raw)
            return parts

        table_scales = keep.tile([P, T], U8, name="table_scales", align_bytes=64)
        nc.gpsimd.memset(table_scales[:].bitcast(I32), 0)
        three_t = load_list(three, "three_t")
        two_t = load_list(two, "two_t")
        offs_t = load_list(offs, "offs_t")
        for q in range(P // QUADRANT):
            nc.sync.dma_start(
                table_scales[QUADRANT * q : QUADRANT * q + 4, :].bitcast(I32),
                x_scales[0, 4 * q : 4 * q + 4, :].bitcast(I32),
            )
        table_words = keep.tile([P, T], U32, name="table_words", align_bytes=64)
        nc.sync.dma_start(table_words[:].bitcast(I32), x_words[0].rearrange("p n t -> p (n t)").bitcast(I32))
        w3_raw = load_weight(w3, "w3_raw", 2)
        n4_t = load_list(n4, "n4_t")
        w2_raw = load_weight(w2, "w2_raw", 2)
        w1_raw = load_weight(w1, "w1_raw", 1)
        n2_t = load_list(n2, "n2_t")
        n3_t = load_list(n3, "n3_t")
        n1_t = load_list(n1, "n1_t")
        ga_t = keep.tile([P, PACK], F32, name="ga_t")
        nc.sync.dma_start(ga_t[:], ga.rearrange("(p t) o -> p (t o)", t=PACK))
        gb_t = keep.tile([P, PACK], F32, name="gb_t")
        nc.sync.dma_start(gb_t[:], gb.rearrange("(p t) o -> p (t o)", t=PACK))
        n5_t = load_list(n5, "n5_t")
        n6_t = load_list(n6, "n6_t")
        n7_t = load_list(n7, "n7_t")

        ident = keep.tile([P, P], F32, name="ident")
        make_identity(nc, ident[:])
        warm = keep.tile([P, 1], F32, name="warm")
        nc.scalar.activation(warm[:], ident[:, 0:1], ACT.Sigmoid)

        def windows(name):
            return [
                keep.tile([P, 2 * W], F32, name="%s%d" % (name, t), tag="%s%d" % (name, t), align_bytes=64)
                for t in range(PACK)
            ]

        b_win, d_win, y_win, s_win = windows("b_win"), windows("d_win"), windows("y_win"), windows("s_win")
        for t in range(PACK):
            nc.gpsimd.memset(b_win[t][:, W:], 0.0)
            nc.gpsimd.memset(y_win[t][:, W:], 0.0)
        b_fetched = [d_win[t][:, W:] for t in range(PACK)]
        b_diff = [s_win[t][:, W:] for t in range(PACK)]

        def pick_scales(offsets, name):
            picked = keep.tile([P, W], U8, name=name, align_bytes=64)
            nc.vector.tensor_copy(picked[:], table_scales[:].indirect(offsets[:]))
            return picked

        def pick_words(offsets, name, tag):
            picked = keep.tile([P, W], U32, name=name, tag=tag, align_bytes=64)
            nc.vector.tensor_copy(picked[:], table_words[:].indirect(offsets[:]))
            return picked

        def quantize_weight(parts, name, tag):
            grouped = keep.tile([P, PACK * W], BF16, name=name + "_grouped", tag=tag, align_bytes=64)
            dealt = grouped[:].rearrange("p (t m j) -> p m j t", t=PACK, j=PACK)
            rows = P // len(parts)
            for h, raw in enumerate(parts):
                nc.scalar.copy(dealt[:, h * rows : (h + 1) * rows], raw[:].rearrange("p j (m t) -> p m j t", t=PACK))
            codes = keep.tile([P, W], U32, name=name + "_codes", align_bytes=64)
            scales = keep.tile([P, W], U8, name=name + "_scales", align_bytes=64)
            nc.vector.quantize_mx(out=codes[:].bitcast(FP8X4), scales=scales[:], in_=grouped[:])
            return codes, scales

        def product(acc, stationary, at, moving, cols=slice(0, W)):
            nc.tensor.matmul_mx(
                out=acc[:, cols],
                lhsT=stationary[0][:, block(at)].bitcast(FP8X4),
                lhsT_scale=stationary[1][:, block(at)],
                rhs=moving[0][:, cols].bitcast(FP8X4),
                rhs_scale=moving[1][:, cols],
                start=True,
                stop=True,
            )

        three_scales = pick_scales(three_t, "three_scales")
        two_scales = pick_scales(two_t, "two_scales")
        offs_scales = pick_scales(offs_t, "offs_scales")
        three_words = pick_words(three_t, "three_words", "three_words")
        two_words = pick_words(two_t, "two_words", "two_words")
        w3_q = quantize_weight(w3_raw, "w3", "w3_grouped")
        offs_words = pick_words(offs_t, "offs_words", "w3_grouped")

        for t in range(PACK):
            acc = bank(t)
            product(acc, w3_q, t, (three_words, three_scales))
            nc.scalar.copy(b_win[t][:, 0:W], acc[:])
        w2_q = quantize_weight(w2_raw, "w2", "w2_grouped")
        for t in range(PACK):
            nc.vector.tensor_copy(b_fetched[t], b_win[t][:].indirect(n4_t[:]))
            nc.gpsimd.tensor_tensor(b_diff[t], b_fetched[t], b_win[t][:, 0:W], ALU.subtract)
        for t in range(PACK):
            acc = bank(PACK + t)
            product(acc, w2_q, t, (two_words, two_scales))
            nc.scalar.copy(d_win[t][:, 0:W], acc[:])
        w1_q = quantize_weight(w1_raw, "w1", "two_words")
        for t in range(PACK):
            acc = bank(t)
            product(acc, w1_q, t, (offs_words, offs_scales))
            nc.scalar.activation(y_win[t][:, 0:W], acc[:], ACT.Copy, scale=ga_t[:, t : t + 1])

        b_rise = keep.tile([P, PACK, W], F32, name="b_rise", tag="w1_raw0")
        b_sig = keep.tile([P, PACK, W], F32, name="b_sig", tag="w3_grouped", align_bytes=64)
        sm = []
        for t in range(PACK):
            nc.scalar.activation(b_rise[:, t, :], b_diff[t], ACT.Relu)
            sm.append(keep.tile([P, W], F32, name="sm%d" % t, tag="sm%d" % t, align_bytes=64))
            nc.gpsimd.tensor_tensor(sm[t][:], b_rise[:, t, :], b_win[t][:, 0:W], ALU.add)

        def scatter_sm(t, tag):
            window = keep.tile([P, 2 * W], F32, name="ds%d" % t, tag=tag, align_bytes=64)
            nc.vector.tensor_copy(window[:].indirect(n3_t[:]), sm[t][:])
            return window

        def gather_and_add_turned(win, offsets, t, banks, fetched):
            nc.vector.tensor_copy(fetched, win[:].indirect(offsets[:]))
            for src, first in ((win, True), (fetched, False)):
                for c in range(PACK):
                    nc.tensor.matmul(
                        banks[c][:, block(t)], src[:, block(c)], ident[:], start=first, stop=not first, is_transpose=True
                    )

        def in_word_order(tile):
            return tile[:].rearrange("j (u p e) -> j u p e", u=2, e=2)

        def from_tile_order(tile):
            return tile[:].rearrange("j (u e p) -> j u p e", u=2, e=2)

        d_banks = [bank(PACK + c) for c in range(PACK)]
        y_banks = [bank(c) for c in range(PACK)]
        d_early = keep.tile([P, 2, W], F32, name="d_early")
        d_late = keep.tile([P, 2, W], F32, name="d_late", tag="two_words", align_bytes=64)
        for t in range(PACK):
            gather_and_add_turned(d_win[t], n2_t, t, d_banks, (d_early, d_late)[t // 2][:, t % 2, :])
        d_gate = []
        for c in range(PACK):
            d_gate.append(keep.tile([P, W], F32, name="d_gate%d" % c, tag="d_gate%d" % c))
            nc.scalar.activation(in_word_order(d_gate[c]), from_tile_order(d_banks[c]), ACT.Sigmoid)
        for t in range(PACK):
            fetched = keep.tile([P, W], F32, name="y_fetched%d" % t, tag="y_fetched%d" % t, align_bytes=64)
            gather_and_add_turned(y_win[t], n1_t, t, y_banks, fetched[:])
        for t in range(PACK):
            nc.scalar.activation(b_sig[:, t, :], b_win[t][:, 0:W], ACT.Sigmoid)
        ds = [scatter_sm(0, "y_win2"), scatter_sm(1, "y_win3"), scatter_sm(2, "y_fetched3")]

        z_grouped = keep.tile([P, PACK * W], BF16, name="z_grouped", align_bytes=64)
        z_words = z_grouped[:].bitcast(F32).rearrange("p (t m u) -> p t m u", t=PACK, u=2)
        per_block = P // PACK
        for c in range(PACK):
            y_sum = keep.tile([P, W], F32, name="y_sum%d" % c, tag="y_sum%d" % c, align_bytes=64)
            nc.scalar.copy(in_word_order(y_sum), from_tile_order(y_banks[c]))
            z_turned = keep.tile([P, W], BF16, name="z_turned%d" % c)
            nc.gpsimd.tensor_tensor(z_turned[:], y_sum[:], d_gate[c][:], ALU.mult)
            back = bank(PACK + c)
            pairs = z_turned[:].bitcast(F32)
            for u in range(2):
                nc.tensor.transpose(back[:, block(u)], pairs[:, block(u)], ident[:])
            nc.scalar.copy(
                z_words[:, :, per_block * c : per_block * (c + 1), :],
                back[:, 0 : 2 * P].rearrange("p (u m t) -> p t m u", u=2, t=PACK),
            )
        ds.append(scatter_sm(LAST, "y_sum0"))

        def quantize_z(first, count, tag):
            name = "z_rows%d" % first
            codes = keep.tile([P, count * P], U32, name=name + "_codes", tag=tag, align_bytes=64)
            scales = keep.tile([P, count * P], U8, name=name + "_scales", align_bytes=64)
            nc.vector.quantize_mx(
                out=codes[:].bitcast(FP8X4), scales=scales[:], in_=z_grouped[:, first * W : (first + count) * W]
            )
            return codes, scales

        z_first = quantize_z(0, 1, "z_first")

        z2_tiles = keep.tile([P, PACK, W], BF16, name="z2_tiles", tag="z2_tiles", align_bytes=64)
        for t in range(LAST):
            weighted = keep.tile([P, W], F32, name="b_weighted%d" % t, tag="d_gate%d" % (t + 1))
            nc.scalar.activation(weighted[:], b_sig[:, t, :], ACT.Copy, scale=gb_t[:, t : t + 1])
            nc.gpsimd.tensor_tensor(z2_tiles[:, t, :], ds[t][:, 0:W], weighted[:], ALU.mult)
        z2_grouped = keep.tile([P, PACK * W], BF16, name="z2_grouped", tag="z2_grouped", align_bytes=64)
        z2_codes = keep.tile([P, W], U32, name="z2_codes", align_bytes=64)
        z2_scales = keep.tile([P, W], U8, name="z2_scales", align_bytes=64)
        z2_q = (z2_codes, z2_scales)
        halves = [slice(0, W // 2), slice(W // 2, W)]
        for cols in halves:
            nc.vector.scalar_tensor_tensor(
                z2_tiles[:, LAST, cols], ds[LAST][:, cols], gb_t[:, LAST:PACK], b_sig[:, LAST, cols], ALU.mult, ALU.mult
            )
        for cols, copy in zip(halves, (nc.scalar.copy, nc.vector.tensor_copy)):
            copy(
                z2_grouped[:, PACK * cols.start : PACK * cols.stop].rearrange("p (c i t) -> p c t i", i=4, t=PACK),
                z2_tiles[:, :, cols].rearrange("p t (c i) -> p c t i", i=4),
            )

        copy_banks = [bank(4), bank(5)]
        sigmoid_banks = [bank(0), bank(6)]
        for h in (1, 0):
            cols = halves[h]
            nc.vector.quantize_mx(
                out=z2_codes[:, cols].bitcast(FP8X4),
                scales=z2_scales[:, cols],
                in_=z2_grouped[:, PACK * cols.start : PACK * cols.stop],
            )
            for acc in (sigmoid_banks[h], copy_banks[h]):
                product(acc, z_first, 0, z2_q, cols)
        z_second = quantize_z(1, 1, "z2_tiles")
        s_banks = {t: bank(t) for t in range(1, PACK)}
        product(s_banks[1], z_second, 0, z2_q)

        out_rows = out.rearrange("(p t) v -> p t v", t=PACK)
        s_sig = [keep.tile([P, W], F32, name="s_sig%d" % t, tag="sm%d" % t, align_bytes=64) for t in range(PACK)]
        far_sig = [keep.tile([P, W], F32, name="far_sig%d" % t) for t in range(PACK)]
        firsts = [keep.tile([P, W], F32, name="first%d" % t) for t in range(PACK)]
        seconds = [keep.tile([P, W], F32, name="second%d" % t) for t in range(PACK)]

        def first_term(t):
            if t == 0:
                for h in (1, 0):
                    cols = halves[h]
                    nc.vector.tensor_scalar(s_win[t][:, cols], copy_banks[h][:, cols], S_FACTOR, None, ALU.mult)
                    nc.scalar.activation(s_sig[t][:, cols], sigmoid_banks[h][:, cols], ACT.Sigmoid, scale=S_FACTOR)
            else:
                nc.scalar.activation(s_win[t][:, 0:W], s_banks[t][:], ACT.Copy, scale=S_FACTOR)
                nc.scalar.activation(s_sig[t][:], s_banks[t][:], ACT.Sigmoid, scale=S_FACTOR)
            nc.vector.tensor_tensor(firsts[t][:], s_win[t][:].indirect(n5_t[:]), s_sig[t][:], ALU.mult)

        def second_term(t, cols):
            entries = n6_t[:, cols.start // GROUP : cols.stop // GROUP]
            nc.vector.tensor_tensor(seconds[t][:, cols], s_win[t][:].indirect(entries), far_sig[t][:, cols], ALU.mult)

        def add_and_store(t, cols):
            total = keep.tile([P, cols.stop - cols.start], F32, name="total%d_%d" % (t, cols.start))
            nc.vector.tensor_tensor(total[:], firsts[t][:, cols], seconds[t][:, cols], ALU.add)
            nc.sync.dma_start(out_rows[:, t, cols], total[:])

        def add_turned_and_store(t):
            there, back = bank(4), bank(5)
            for c in range(PACK):
                for src, first in ((firsts[t], True), (seconds[t], False)):
                    nc.tensor.matmul(
                        there[:, block(c)], src[:, block(c)], ident[:], start=first, stop=not first, is_transpose=True
                    )
            turned = keep.tile([P, W], F32, name="turned", tag="y_sum1", align_bytes=64)
            nc.scalar.copy(turned[:], there[:])
            for c in range(PACK):
                nc.tensor.transpose(back[:, block(c)], turned[:, block(c)], ident[:])
            total = keep.tile([P, W], F32, name="total_turned")
            nc.scalar.copy(total[:], back[:])
            nc.sync.dma_start(out_rows[:, t, :], total[:])

        first_term(0)
        z_rest = quantize_z(2, 2, "z2_grouped")
        for t in (2, 3):
            product(s_banks[t], z_rest, t - 2, z2_q)
        whole = slice(0, W)
        ending = [slice(0, 3 * W // 4), slice(3 * W // 4, W)]
        for t in range(PACK):
            if t < LAST:
                first_term(t + 1)
            nc.scalar.activation(far_sig[t][:], s_win[t][:].indirect(n7_t[:]), ACT.Sigmoid)
            second_term(t, whole if t < LAST else ending[0])
            if t == LAST - 1:
                add_turned_and_store(0)
            if t > 1:
                add_and_store(t - 1, whole)
        second_term(LAST, ending[1])
        for cols in ending:
            add_and_store(LAST, cols)
